import numpy as np
import ml_dtypes


def mxq(x, axis, fmt="e4m3"):
    dtype, down = {"e4m3": (ml_dtypes.float8_e4m3fn, 7), "e5m2": (ml_dtypes.float8_e5m2, 14)}[fmt]
    v = np.moveaxis(np.asarray(x, np.float32).astype(ml_dtypes.bfloat16).astype(np.float64), axis, -1)
    blocks = v.reshape(v.shape[:-1] + (-1, 32))
    amax = np.abs(blocks).max(-1, keepdims=True)
    byte = np.maximum(np.where(amax > 0, np.frexp(amax)[1] - 1 + 127, 0) - down, 1)
    scale = np.exp2(byte - 127.0)
    codes = (blocks / scale).astype(np.float32).astype(dtype).astype(np.float64)
    return np.moveaxis((codes * scale).reshape(v.shape), -1, axis)


WIDE = False


def mx_kscale(k):
    if not WIDE:
        return np.ones(k)
    levels = np.array([10, -10, 5, -5, 0])
    if k % 512:
        return np.exp2(np.random.permutation(np.resize(levels, k // 32))).repeat(32)
    a = np.empty((k // 512, 16))
    for p in range(k // 512):
        a[p, :8] = np.random.permutation(np.resize(levels, 8))
        for g in range(8):
            far = levels[np.abs(levels - a[p, g]) >= 10]
            a[p, g + 8] = far[np.random.randint(len(far))]
    return np.exp2(a.ravel()).repeat(32)


BF16 = ml_dtypes.bfloat16


def bf(x):
    return np.asarray(x, np.float32).astype(BF16)


def f64(x):
    return np.asarray(x).astype(np.float64)

def planes(Y):
    n, m = Y.shape
    b = f64(bf(Y)).reshape(n // 32, 32, m)
    amax = np.abs(b).max(1)
    byte = np.clip(np.where(amax > 0, np.frexp(amax)[1] - 1 + 127 - 7, 1), 1, 254)
    codes = (b * np.exp2(127.0 - byte)[:, None, :]).reshape(n, m).astype(np.float32).astype(ml_dtypes.float8_e4m3fn).view(np.uint8)
    words = codes.reshape(n // 512, 128, 4, m).transpose(0, 1, 3, 2)
    return np.ascontiguousarray(words), np.ascontiguousarray(byte.astype(np.uint8).reshape(n // 512, 16, m))


N, D, H, P = 1024, 1024, 1024, 2

LOSS_DIV = 32.0


def hidden_input(vw, scale, b):
    return scale[:, None] * vw + b[None, :]


def hidden_signal(a, scale, lam):
    return scale[:, None] * (lam[None, :] - 1.0 / (1.0 + np.exp(-a)))


def setup_inputs():
    s = mx_kscale(D)
    rp, rn = mx_kscale(N), mx_kscale(N)
    return {
        "vpos": bf(np.random.standard_normal((N, D)) * s[None, :] * rp[:, None]),
        "vneg": bf(np.random.standard_normal((N, D)) * s[None, :] * rn[:, None]),
        "beta": bf((1.0 + 0.1 * np.random.standard_normal((P, N))) / np.stack([rp, rn])),
        "u": bf(np.random.standard_normal((D, H)) / np.sqrt(D)),
        "c": bf((1.0 + 0.1 * np.random.standard_normal(D)) / s),
        "b": bf(np.random.standard_normal(H) * 0.5),
        "lam": bf(np.random.uniform(0.2, 0.8, H)),
    }


def core(vpos, vneg, beta, u, c, b, lam):
    vp, vn, be, cc, bb, ll = f64(vpos), f64(vneg), f64(beta), f64(c), f64(b), f64(lam)
    wm = mxq(cc[:, None] * f64(u), 0, "e4m3")
    ap = hidden_input(mxq(vp, 1, "e4m3") @ wm, be[0], bb)
    an = hidden_input(mxq(vn, 1, "e4m3") @ wm, be[1], bb)
    gp = hidden_signal(ap, be[0], ll)
    gn = hidden_signal(an, be[1], ll)
    m = (mxq(vp, 0, "e4m3").T @ mxq(gp, 0, "e4m3")) - (mxq(vn, 0, "e4m3").T @ mxq(gn, 0, "e4m3"))
    return cc[:, None] * m / LOSS_DIV


def reference(vpos, vneg, beta, u, c, b, lam):
    R_out = core(vpos, vneg, beta, u, c, b, lam)
    words, scales = planes(R_out)
    return R_out, words, scales

@@ -1,0 +1,660 @@
+from contextlib import ExitStack
+
+import concourse.mybir as mybir
+from concourse.masks import make_identity
+
+F32 = mybir.dt.float32
+BF16 = mybir.dt.bfloat16
+U32 = mybir.dt.uint32
+I32 = mybir.dt.int32
+U8 = mybir.dt.uint8
+FP8X4 = mybir.dt.float8_e4m3fn_x4
+ALU = mybir.AluOpType
+ACT = mybir.ActivationFunctionType
+
+N = D = H = 1024
+P = 128
+PACK = 4
+KP = P * PACK
+GROUPS = 2
+CHUNK = 256
+CHUNKS = H // CHUNK
+BLOCKS = 4
+UNITS = CHUNKS * BLOCKS
+LOSS_DIV = 32.0
+
+TR_BUFS = 2
+ACC_BUFS = 2
+WB = {"pool": 1, "act": 3, "dve": 2}
+
+FLOPS = 4 * 2 * N * D * H
+
+
+def tile_gaussianrbmtwophasehiddenoffsetgrad_x1_kernel(tc, vpos, vneg, beta, u, c, b, lam, out_0, out_1, out_2):
+    nc = tc.nc
+    with ExitStack() as ctx:
+        keep = ctx.enter_context(tc.tile_pool(name="keep", bufs=1))
+        work = ctx.enter_context(tc.tile_pool(name="work", bufs=2))
+        psum = ctx.enter_context(tc.psum_pool(name="psum", bufs=2))
+        ctx.enter_context(tc.manual_schedule())
+
+        def kept(name, shape, dtype):
+            return keep.tile(shape, dtype, name=name, align_bytes=64)
+
+        ident_f = kept("ident_f", [P, P], F32)
+        ident_b = kept("ident_b", [P, P], BF16)
+        c_raw = kept("c_raw", [P, GROUPS, PACK], BF16)
+        c_in = kept("c_in", [P, GROUPS * PACK], F32)
+        c_out = kept("c_out", [P, GROUPS * PACK], F32)
+        beta_raw = kept("beta_raw", [P, BLOCKS, PACK], BF16)
+        beta_sgn = kept("beta_sgn", [P, BLOCKS * PACK], BF16)
+        beta_row = kept("beta_row", [P, BLOCKS, KP], BF16)
+        bl_rows = kept("bl_rows", [P, P], BF16)
+        bl_col = kept("bl_col", [P, 16], F32)
+        warm = kept("warm", [P, 1], F32)
+        u_raw = [kept("u_raw%d" % i, [P, GROUPS, PACK, CHUNK], BF16) for i in range(CHUNKS)]
+        v_raw = [kept("v_raw%d" % i, [P, PACK, D], BF16) for i in range(BLOCKS)]
+        vd_codes = [kept("vd_codes%d" % i, [P, GROUPS, KP], U32) for i in range(BLOCKS)]
+        vd_scales = [kept("vd_scales%d" % i, [P, GROUPS, KP], U8) for i in range(BLOCKS)]
+        vn_codes = [kept("vn_codes%d" % i, [P, GROUPS, KP], U32) for i in range(BLOCKS)]
+        vn_scales = [kept("vn_scales%d" % i, [P, GROUPS, KP], U8) for i in range(BLOCKS)]
+        w_codes = [kept("w_codes%d" % i, [P, GROUPS, CHUNK], U32) for i in range(CHUNKS)]
+        w_scales = [kept("w_scales%d" % i, [P, GROUPS, CHUNK], U8) for i in range(CHUNKS)]
+        g_codes = [kept("g_codes%d" % i, [P, H], U32) for i in range(BLOCKS)]
+        g_scales = [kept("g_scales%d" % i, [P, H], U8) for i in range(BLOCKS)]
+        o_codes = kept("o_codes", [P, GROUPS, H], U32)
+        o_scales = kept("o_scales", [P, GROUPS, H], U8)
+        live = {}
+
+        def v_rows(i):
+            src = vpos if i < GROUPS else vneg
+            g = i % GROUPS
+            return src[g * KP:(g + 1) * KP, :].rearrange("(p j) d -> p j d", j=PACK)
+
+        def load_u(hc):
+            cols = slice(hc * CHUNK, (hc + 1) * CHUNK)
+            for g in range(GROUPS):
+                nc.sync.dma_start(out=u_raw[hc][:, g, :, :], in_=u[g * KP:(g + 1) * KP, cols].rearrange("(p j) h -> p j h", j=PACK))
+
+        def loads():
+            nc.vector.memset(warm[:], 0.0)
+            nc.vector.memset(bl_rows[:], 0.0)
+            make_identity(nc, ident_f[:])
+            make_identity(nc, ident_b[:])
+            nc.sync.dma_start(out=v_raw[0][:, :, 0:KP], in_=v_rows(0)[:, :, 0:KP])
+            nc.scalar.dma_start(out=c_raw[:], in_=c.rearrange("(g p j) -> p g j", g=GROUPS, j=PACK))
+            nc.scalar.dma_start(out=beta_raw[:], in_=beta.rearrange("f (g p j) -> p (f g) j", g=GROUPS, j=PACK))
+            nc.scalar.dma_start(out=bl_rows[0:8, :], in_=b.rearrange("(r m) -> r m", m=P))
+            nc.scalar.dma_start(out=bl_rows[8:16, :], in_=lam.rearrange("(r m) -> r m", m=P))
+            nc.scalar.activation(out=warm[:], in_=warm[:], func=ACT.Sigmoid)
+            load_u(0)
+            nc.sync.dma_start(out=v_raw[0][:, :, KP:D], in_=v_rows(0)[:, :, KP:D])
+            nc.sync.dma_start(out=v_raw[1][:], in_=v_rows(1))
+            load_u(1)
+            nc.sync.dma_start(out=v_raw[2][:], in_=v_rows(2))
+            nc.sync.dma_start(out=v_raw[3][:], in_=v_rows(3))
+            load_u(2)
+            load_u(3)
+
+        def small_vector():
+            flat_c = c_raw[:].rearrange("p g j -> p (g j)")
+            nc.vector.tensor_copy(out=c_in[:], in_=flat_c)
+            nc.vector.tensor_scalar(out=c_out[:], in0=flat_c, scalar1=1.0 / LOSS_DIV, scalar2=None, op0=ALU.mult)
+            flat_b = beta_raw[:].rearrange("p i j -> p (i j)")
+            nc.vector.tensor_scalar(out=beta_sgn[:, 0:8], in0=flat_b[:, 0:8], scalar1=-1.0, scalar2=None, op0=ALU.mult)
+            nc.vector.tensor_copy(out=beta_sgn[:, 8:16], in_=flat_b[:, 8:16])
+
+        def spread_beta(ph):
+            bank = psum.tile([P, 4, P], F32, name="beta_bank", bufs=2)
+            live["beta_bank", ph] = bank
+            words = beta_sgn[:].bitcast(F32)
+            for k in range(4):
+                w = 4 * ph + k
+                nc.tensor.transpose(bank[:, k, :], words[:, w:w + 1].to_broadcast([P, P]), ident_f[:])
+
+        def beta_out(ph):
+            bank = live["beta_bank", ph]
+            dst = beta_row[:, GROUPS * ph:GROUPS * (ph + 1), :].rearrange("p i n -> p (i n)").bitcast(F32)
+            nc.scalar.copy(out=dst, in_=bank[:].rearrange("p k q -> p (k q)"))
+
+        def spread_bl():
+            bank = psum.tile([P, P], BF16, name="tr", bufs=TR_BUFS)
+            nc.tensor.transpose(bank[:], bl_rows[:], ident_b[:])
+            live["bl_bank"] = bank
+
+        def bl_out():
+            nc.scalar.copy(out=bl_col[:], in_=live["bl_bank"][:, 0:16])
+
+        def pool_copy(out, in_):
+            nc.gpsimd.tensor_scalar(out=out, in0=in_, scalar1=1.0, scalar2=0.0, op0=ALU.mult, op1=ALU.add)
+
+        def act_copy(out, in_):
+            nc.scalar.copy(out=out, in_=in_)
+
+        def dve_copy(out, in_):
+            nc.vector.tensor_copy(out=out, in_=in_)
+
+        def lane(copy):
+            return "pool" if copy is pool_copy else "act" if copy is act_copy else "dve"
+
+        def w_scale(hc):
+            scaled = work.tile([P, GROUPS, PACK, CHUNK], BF16, name="w_scaled", bufs=1)
+            for g in range(GROUPS):
+                for j in range(PACK):
+                    k = PACK * g + j
+                    nc.vector.tensor_scalar(out=scaled[:, g, j, :], in0=u_raw[hc][:, g, j, :], scalar1=c_in[:, k:k + 1], scalar2=None, op0=ALU.mult)
+            live["w_scaled", hc] = scaled
+
+        def w_weave(hc, copy):
+            woven = work.tile([P, GROUPS, CHUNK, PACK], BF16, name="woven_" + lane(copy), bufs=WB[lane(copy)], align_bytes=64)
+            copy(out=woven[:], in_=live["w_scaled", hc][:].rearrange("p g j h -> p g h j"))
+            live["w_woven", hc] = woven
+
+        def w_quant(hc):
+            nc.vector.quantize_mx(
+                out=w_codes[hc][:].rearrange("p g h -> p (g h)").bitcast(FP8X4),
+                scales=w_scales[hc][:].rearrange("p g h -> p (g h)"),
+                in_=live["w_woven", hc][:].rearrange("p g h j -> p (g h j)"))
+
+        def vd_turn(i, g, half):
+            bank = psum.tile([P, 2, 2, P], F32, name="tr", bufs=TR_BUFS)
+            for e in range(2):
+                words = v_raw[i][:, 2 * half + e, :].bitcast(F32)
+                for w in range(2):
+                    nc.tensor.transpose(bank[:, e, w, :], words[:, 256 * g + w:256 * (g + 1):2], ident_f[:])
+            live["vd_bank", i, g, half] = bank
+
+        def vd_out(i, g, half):
+            if half == 0:
+                live["vd_woven", i, g] = work.tile([P, 2, P, 2, 2], F32, name="vd_woven", bufs=2, align_bytes=64)
+            nc.scalar.copy(out=live["vd_woven", i, g][:, half, :, :, :], in_=live["vd_bank", i, g, half][:].rearrange("p e w q -> p q e w"))
+
+        def vd_quant(i, g):
+            nc.vector.quantize_mx(out=vd_codes[i][:, g, :].bitcast(FP8X4), scales=vd_scales[i][:, g, :],
+                                  in_=live["vd_woven", i, g][:].rearrange("p a q e w -> p (a q e w)").bitcast(BF16))
+
+        def vn_weave(i, g, half, copy):
+            if half == 0:
+                live["vn_woven", i, g] = work.tile([P, PACK, P, PACK], BF16, name="woven_" + lane(copy), bufs=WB[lane(copy)], align_bytes=64)
+            parts = 2 if copy is act_copy else 1
+            ms = slice(half * P // parts, (half + 1) * P // parts)
+            woven = live["vn_woven", i, g][:, :, ms, :]
+            src = v_raw[i][:, :, g * KP + PACK * ms.start:g * KP + PACK * ms.stop]
+            if copy is pool_copy:
+                copy(out=woven.rearrange("p t m j -> p m j t"), in_=src.rearrange("p j (m t) -> p m j t", t=PACK))
+            else:
+                copy(out=woven.rearrange("p t (m a) j -> p m t a j", a=2), in_=src.rearrange("p j (m a t) -> p m t a j", a=2, t=PACK))
+
+        def vn_quant(i, g):
+            nc.vector.quantize_mx(out=vn_codes[i][:, g, :].bitcast(FP8X4), scales=vn_scales[i][:, g, :],
+                                  in_=live["vn_woven", i, g][:].rearrange("p t m j -> p (t m j)"))
+
+        def hidden_mm(un, a):
+            hc, i = divmod(un, BLOCKS)
+            acc = psum.tile([P, KP], F32, name="acc", bufs=ACC_BUFS)
+            cols = slice(a * P, (a + 1) * P)
+            for g in range(GROUPS):
+                nc.tensor.matmul_mx(out=acc[:], lhsT=w_codes[hc][:, g, cols].bitcast(FP8X4), lhsT_scale=w_scales[hc][:, g, cols],
+                                    rhs=vd_codes[i][:, g, :].bitcast(FP8X4), rhs_scale=vd_scales[i][:, g, :],
+                                    start=(g == 0), stop=(g == GROUPS - 1))
+            live["acc", un, a] = acc
+
+        def hidden_beta(un, a):
+            z = work.tile([P, KP], F32, name="z", bufs=4)
+            nc.vector.tensor_tensor(out=z[:], in0=live["acc", un, a][:], in1=beta_row[:, un % BLOCKS, :], op=ALU.mult)
+            live["z", un, a] = z
+
+        def hidden_sigmoid(un, a):
+            hc, i = divmod(un, BLOCKS)
+            ht = 2 * hc + a
+            s = work.tile([P, KP], F32, name="s", bufs=4)
+            nc.scalar.activation(out=s[:], in_=live["z", un, a][:], func=ACT.Sigmoid, bias=bl_col[:, ht:ht + 1], scale=(-1.0 if i < GROUPS else 1.0))
+            live["s", un, a] = s
+
+        def beta_psum(i):
+            ph, g = divmod(i, GROUPS)
+            return live["beta_bank", ph][:, 2 * g:2 * g + 2, :].rearrange("p k q -> p (k q)").bitcast(BF16)
+
+        def hidden_signal(un, a):
+            hc, i = divmod(un, BLOCKS)
+            ht = 2 * hc + a
+            gt = work.tile([P, KP], BF16, name="gt", bufs=4)
+            nc.vector.scalar_tensor_tensor(out=gt[:], in0=live["s", un, a][:], scalar=bl_col[:, 8 + ht:9 + ht], in1=beta_psum(i),
+                                           op0=ALU.subtract, op1=ALU.mult)
+            live["gt", un, a] = gt
+
+        def g_turn(un):
+            bank = psum.tile([P, 2, 2, P], F32, name="tr", bufs=TR_BUFS)
+            for a in range(2):
+                words = live["gt", un, a][:].bitcast(F32)
+                for w in range(2):
+                    nc.tensor.transpose(bank[:, a, w, :], words[:, w * P:(w + 1) * P], ident_f[:])
+            live["g_bank", un] = bank
+
+        def g_out(un):
+            woven = work.tile([P, 2, P, 2], F32, name="g_woven", bufs=3, align_bytes=64)
+            nc.scalar.copy(out=woven[:], in_=live["g_bank", un][:].rearrange("p a w h -> p a h w"))
+            live["g_woven", un] = woven
+
+        def g_quant(un):
+            hc, i = divmod(un, BLOCKS)
+            cols = slice(hc * CHUNK, (hc + 1) * CHUNK)
+            nc.vector.quantize_mx(out=g_codes[i][:, cols].bitcast(FP8X4), scales=g_scales[i][:, cols],
+                                  in_=live["g_woven", un][:].rearrange("p a h w -> p (a h w)").bitcast(BF16))
+
+        def grad_mm(hc, g, t, blocks=range(BLOCKS), tag="oacc"):
+            if blocks[0] == 0:
+                live["oacc", hc, g, t] = psum.tile([P, CHUNK], F32, name=tag, bufs=2)
+            acc = live["oacc", hc, g, t]
+            rows = slice(t * P, (t + 1) * P)
+            cols = slice(hc * CHUNK, (hc + 1) * CHUNK)
+            for i in blocks:
+                nc.tensor.matmul_mx(out=acc[:], lhsT=vn_codes[i][:, g, rows].bitcast(FP8X4), lhsT_scale=vn_scales[i][:, g, rows],
+                                    rhs=g_codes[i][:, cols].bitcast(FP8X4), rhs_scale=g_scales[i][:, cols],
+                                    start=(i == 0), stop=(i == BLOCKS - 1))
+
+        def grad_out(hc, g, t, on="act"):
+            if t == 0:
+                live["res", hc, g] = work.tile([P, PACK, CHUNK], F32, name="res", bufs=3)
+            k = PACK * g + t
+            if on == "act":
+                nc.scalar.activation(out=live["res", hc, g][:, t, :], in_=live["oacc", hc, g, t][:], func=ACT.Copy, scale=c_out[:, k:k + 1])
+            else:
+                nc.vector.tensor_scalar(out=live["res", hc, g][:, t, :], in0=live["oacc", hc, g, t][:], scalar1=c_out[:, k:k + 1], scalar2=None, op0=ALU.mult)
+
+        def grad_store(hc, g):
+            cols = slice(hc * CHUNK, (hc + 1) * CHUNK)
+            nc.sync.dma_start(out=out_0[g * KP:(g + 1) * KP, cols].rearrange("(p t) m -> p t m", t=PACK), in_=live["res", hc, g][:])
+
+        def grad_weave(hc, g, copy):
+            woven = work.tile([P, CHUNK, PACK], BF16, name="res_woven_%s%d" % (lane(copy), g), bufs=1, align_bytes=64)
+            copy(out=woven[:], in_=live["res", hc, g][:].rearrange("p t m -> p m t"))
+            live["res_woven", hc, g] = woven
+
+        def grad_quant(hc, g):
+            cols = slice(hc * CHUNK, (hc + 1) * CHUNK)
+            nc.vector.quantize_mx(out=o_codes[:, g, cols].bitcast(FP8X4), scales=o_scales[:, g, cols],
+                                  in_=live["res_woven", hc, g][:].rearrange("p m t -> p (m t)"))
+
+        def code_store(hc, g):
+            cols = slice(hc * CHUNK, (hc + 1) * CHUNK)
+            nc.sync.dma_start(out=out_1[g, :, cols, :].rearrange("p m t -> p (m t)").bitcast(I32), in_=o_codes[:, g, cols].bitcast(I32))
+
+        def scale_store(lo, hi, queues):
+            for q in range(4):
+                queues[q % len(queues)].dma_start(
+                    out=out_2[:, 4 * q:4 * q + 4, lo:hi].rearrange("g r m -> r g m").bitcast(I32),
+                    in_=o_scales[32 * q:32 * q + 4, :, lo:hi].bitcast(I32))
+
+        def scale_store_a():
+            scale_store(0, 768, [nc.sync])
+
+        def scale_store_b():
+            scale_store(768, 1024, [nc.sync, nc.scalar])
+
+        G, A, V = pool_copy, act_copy, dve_copy
+        loads()
+        small_vector()
+        vd_turn(0, 0, 0)
+        vn_weave(0, 0, 0, V)
+        spread_beta(0)
+        spread_beta(1)
+        vd_out(0, 0, 0)
+        vd_turn(0, 0, 1)
+        beta_out(0)
+        w_scale(0)
+        beta_out(1)
+        w_weave(0, V)
+        vd_out(0, 0, 1)
+        vd_turn(0, 1, 0)
+        vn_weave(0, 1, 0, A)
+        vd_turn(0, 1, 1)
+        vd_quant(0, 0)
+        w_quant(0)
+        vd_out(0, 1, 0)
+        vn_quant(0, 0)
+        vd_out(0, 1, 1)
+        vd_turn(1, 1, 0)
+        vn_weave(1, 0, 0, A)
+        vd_quant(0, 1)
+        vd_turn(1, 1, 1)
+        hidden_mm(0, 0)
+        w_scale(1)
+        vd_out(1, 1, 0)
+        hidden_mm(0, 1)
+        hidden_beta(0, 0)
+        vd_out(1, 1, 1)
+        vd_turn(1, 0, 0)
+        w_weave(1, V)
+        vn_weave(1, 0, 1, A)
+        spread_bl()
+        hidden_beta(0, 1)
+        vd_out(1, 0, 0)
+        w_quant(1)
+        bl_out()
+        vn_weave(1, 1, 0, A)
+        vd_turn(1, 0, 1)
+        vn_quant(1, 0)
+        hidden_mm(4, 0)
+        vd_quant(1, 1)
+        hidden_sigmoid(0, 0)
+        hidden_mm(4, 1)
+        hidden_beta(4, 0)
+        vd_out(1, 0, 1)
+        vd_turn(2, 1, 0)
+        hidden_signal(0, 0)
+        hidden_sigmoid(0, 1)
+        vd_turn(2, 1, 1)
+        vd_quant(1, 0)
+        hidden_sigmoid(4, 0)
+        hidden_beta(4, 1)
+        vd_out(2, 1, 0)
+        hidden_mm(1, 0)
+        w_scale(2)
+        vd_out(2, 1, 1)
+        hidden_mm(1, 1)
+        vn_weave(0, 1, 1, A)
+        hidden_beta(1, 0)
+        vd_turn(2, 0, 0)
+        vd_quant(2, 1)
+        vd_turn(2, 0, 1)
+        hidden_signal(0, 1)
+        vd_out(2, 0, 0)
+        hidden_mm(5, 0)
+        hidden_beta(1, 1)
+        vd_out(2, 0, 1)
+        vd_turn(3, 0, 0)
+        hidden_signal(4, 0)
+        hidden_sigmoid(1, 0)
+        vd_quant(2, 0)
+        g_turn(0)
+        hidden_sigmoid(1, 1)
+        hidden_mm(5, 1)
+        hidden_beta(5, 0)
+        vd_out(3, 0, 0)
+        vn_quant(0, 1)
+        g_out(0)
+        vd_turn(3, 0, 1)
+        hidden_signal(1, 1)
+        hidden_sigmoid(4, 1)
+        hidden_mm(2, 1)
+        g_quant(0)
+        vn_weave(2, 1, 0, A)
+        hidden_signal(4, 1)
+        vd_turn(3, 1, 0)
+        hidden_beta(5, 1)
+        vd_out(3, 0, 1)
+        hidden_beta(2, 1)
+        hidden_mm(2, 0)
+        vd_out(3, 1, 0)
+        hidden_signal(1, 0)
+        hidden_mm(6, 0)
+        hidden_sigmoid(2, 1)
+        vd_quant(3, 0)
+        vd_turn(3, 1, 1)
+        hidden_sigmoid(5, 0)
+        hidden_beta(2, 0)
+        hidden_sigmoid(5, 1)
+        g_turn(4)
+        hidden_beta(6, 0)
+        vd_out(3, 1, 1)
+        hidden_signal(2, 1)
+        hidden_sigmoid(2, 0)
+        w_weave(2, V)
+        g_turn(1)
+        vn_weave(3, 1, 0, A)
+        hidden_mm(6, 1)
+        vd_quant(3, 1)
+        hidden_mm(3, 0)
+        g_out(4)
+        hidden_signal(5, 0)
+        vn_weave(1, 1, 1, A)
+        hidden_beta(6, 1)
+        hidden_signal(5, 1)
+        hidden_mm(3, 1)
+        hidden_sigmoid(6, 0)
+        hidden_beta(3, 0)
+        vn_weave(2, 1, 1, A)
+        hidden_beta(3, 1)
+        hidden_mm(7, 1)
+        hidden_signal(2, 0)
+        hidden_mm(7, 0)
+        vn_quant(1, 1)
+        hidden_sigmoid(3, 0)
+        g_turn(2)
+        hidden_beta(7, 1)
+        hidden_sigmoid(6, 1)
+        hidden_signal(3, 0)
+        hidden_sigmoid(3, 1)
+        w_quant(2)
+        g_out(1)
+        g_quant(4)
+        vn_weave(2, 0, 0, A)
+        hidden_beta(7, 0)
+        g_turn(5)
+        hidden_mm(8, 0)
+        w_scale(3)
+        hidden_mm(8, 1)
+        g_out(2)
+        hidden_signal(6, 0)
+        g_out(5)
+        g_quant(1)
+        g_quant(2)
+        vn_weave(3, 1, 1, A)
+        hidden_signal(3, 1)
+        g_turn(3)
+        hidden_signal(6, 1)
+        g_turn(6)
+        vn_quant(2, 1)
+        hidden_sigmoid(7, 0)
+        hidden_beta(8, 0)
+        hidden_sigmoid(7, 1)
+        hidden_beta(8, 1)
+        g_out(3)
+        hidden_mm(10, 1)
+        g_quant(5)
+        hidden_sigmoid(8, 0)
+        g_quant(3)
+        g_out(6)
+        vn_quant(3, 1)
+        grad_mm(0, 1, 0)
+        vn_weave(3, 0, 0, A)
+        hidden_signal(7, 0)
+        grad_mm(0, 1, 1)
+        hidden_beta(10, 1)
+        hidden_mm(10, 0)
+        hidden_signal(7, 1)
+        hidden_sigmoid(8, 1)
+        g_turn(7)
+        hidden_signal(8, 0)
+        grad_out(0, 1, 0)
+        hidden_sigmoid(10, 1)
+        hidden_signal(8, 1)
+        grad_mm(0, 1, 3)
+        grad_out(0, 1, 1)
+        g_quant(6)
+        g_out(7)
+        hidden_beta(10, 0)
+        hidden_mm(9, 1)
+        vn_weave(2, 0, 1, A)
+        g_turn(8)
+        g_quant(7)
+        grad_mm(1, 1, 0)
+        hidden_beta(9, 1)
+        w_weave(3, V)
+        hidden_mm(9, 0)
+        grad_out(0, 1, 3)
+        grad_out(1, 1, 0)
+        grad_mm(0, 1, 2)
+        hidden_sigmoid(10, 0)
+        hidden_beta(9, 0)
+        hidden_mm(11, 1)
+        vn_weave(3, 0, 1, A)
+        w_quant(3)
+        grad_mm(1, 1, 3)
+        hidden_beta(11, 1)
+        hidden_mm(11, 0)
+        grad_out(0, 1, 2)
+        grad_out(1, 1, 3)
+        vn_quant(2, 0)
+        grad_mm(1, 1, 1)
+        grad_store(0, 1)
+        g_out(8)
+        vn_quant(3, 0)
+        hidden_mm(15, 0)
+        hidden_sigmoid(9, 1)
+        hidden_signal(10, 1)
+        grad_mm(0, 0, 0)
+        grad_out(1, 1, 1)
+        hidden_beta(11, 0)
+        hidden_sigmoid(9, 0)
+        grad_mm(0, 0, 2)
+        hidden_beta(15, 0)
+        grad_out(0, 0, 0)
+        grad_weave(0, 1, A)
+        hidden_signal(9, 1)
+        grad_mm(1, 0, 0)
+        hidden_signal(10, 0)
+        hidden_mm(15, 1)
+        hidden_signal(9, 0)
+        grad_out(0, 0, 2)
+        hidden_mm(12, 1)
+        hidden_sigmoid(11, 1)
+        grad_mm(1, 0, 3)
+        grad_out(1, 0, 0)
+        hidden_beta(12, 1)
+        hidden_sigmoid(11, 0)
+        g_turn(10)
+        g_quant(8)
+        g_turn(9)
+        grad_out(1, 0, 3)
+        hidden_beta(15, 1)
+        grad_mm(1, 0, 2)
+        hidden_sigmoid(15, 0)
+        hidden_signal(11, 1)
+        g_out(9)
+        grad_mm(1, 1, 2)
+        hidden_signal(11, 0)
+        g_out(10)
+        hidden_mm(12, 0)
+        hidden_signal(15, 0)
+        grad_out(1, 1, 2)
+        hidden_mm(13, 1)
+        hidden_beta(12, 0)
+        grad_out(1, 0, 2)
+        g_turn(11)
+        grad_store(1, 1)
+        hidden_sigmoid(15, 1)
+        hidden_beta(13, 1)
+        grad_mm(0, 0, 3)
+        hidden_sigmoid(12, 1)
+        hidden_signal(15, 1)
+        grad_mm(0, 0, 1)
+        hidden_sigmoid(12, 0)
+        grad_weave(1, 1, V)
+        hidden_mm(13, 0)
+        grad_out(0, 0, 3)
+        g_out(11)
+        g_quant(10)
+        grad_mm(1, 0, 1)
+        hidden_beta(13, 0)
+        grad_out(0, 0, 1)
+        g_turn(15)
+        hidden_sigmoid(13, 1)
+        hidden_signal(12, 1)
+        hidden_mm(14, 0)
+        grad_out(1, 0, 1)
+        g_quant(9)
+        grad_weave(0, 0, A)
+        g_quant(11)
+        hidden_mm(14, 1)
+        grad_store(1, 0)
+        grad_store(0, 0)
+        hidden_signal(12, 0)
+        grad_mm(2, 0, 0)
+        hidden_beta(14, 1)
+        hidden_sigmoid(13, 0)
+        grad_mm(2, 0, 2)
+        hidden_beta(14, 0)
+        grad_out(2, 0, 0)
+        g_turn(12)
+        hidden_signal(13, 0)
+        g_out(15)
+        grad_mm(2, 0, 3)
+        hidden_signal(13, 1)
+        grad_out(2, 0, 2)
+        hidden_sigmoid(14, 1)
+        grad_mm(2, 0, 1)
+        grad_out(2, 0, 3)
+        hidden_signal(14, 1)
+        g_turn(13)
+        hidden_sigmoid(14, 0)
+        grad_mm(2, 1, 0)
+        g_quant(15)
+        grad_out(2, 0, 1)
+        hidden_signal(14, 0)
+        g_out(12)
+        grad_mm(2, 1, 1)
+        grad_quant(0, 0)
+        grad_out(2, 1, 0)
+        grad_weave(2, 0, V)
+        g_turn(14)
+        g_out(13)
+        code_store(0, 0)
+        grad_store(2, 0)
+        grad_mm(2, 1, 3)
+        grad_out(2, 1, 1)
+        grad_quant(0, 1)
+        g_out(14)
+        g_quant(13)
+        grad_mm(2, 1, 2)
+        code_store(0, 1)
+        g_quant(12)
+        grad_out(2, 1, 3)
+        g_quant(14)
+        grad_mm(3, 1, 0, range(3), "beta_bank")
+        grad_out(2, 1, 2)
+        grad_quant(1, 1)
+        grad_weave(1, 0, A)
+        grad_quant(2, 0)
+        grad_mm(3, 1, 0, range(3, 4))
+        grad_mm(3, 1, 2, range(3), "tr")
+        code_store(1, 1)
+        grad_weave(2, 1, V)
+        grad_store(2, 1)
+        code_store(2, 0)
+        grad_mm(3, 1, 3, range(3), "tr")
+        grad_mm(3, 1, 2, range(3, 4))
+        grad_mm(3, 1, 1, range(3), "beta_bank")
+        grad_quant(2, 1)
+        grad_quant(1, 0)
+        grad_out(3, 1, 0, "act")
+        grad_mm(3, 1, 1, range(3, 4))
+        grad_mm(3, 1, 3, range(3, 4))
+        grad_out(3, 1, 2, "act")
+        grad_mm(3, 0, 3, range(3), "acc")
+        grad_out(3, 1, 1, "dve")
+        scale_store_a()
+        grad_out(3, 1, 3, "act")
+        grad_mm(3, 0, 3, range(3, 4))
+        grad_mm(3, 0, 0, range(3), "oacc")
+        code_store(1, 0)
+        grad_weave(3, 1, V)
+        grad_store(3, 1)
+        grad_mm(3, 0, 0, range(3, 4))
+        grad_mm(3, 0, 1, range(3), "oacc")
+        grad_out(3, 0, 0, "act")
+        grad_mm(3, 0, 2, range(3), "acc")
+        grad_out(3, 0, 3, "dve")
+        code_store(2, 1)
+        grad_quant(3, 1)
+        grad_mm(3, 0, 2, range(3, 4))
+        grad_mm(3, 0, 1, range(3, 4))
+        grad_out(3, 0, 2, "act")
+        code_store(3, 1)
+        grad_out(3, 0, 1, "dve")
+        grad_weave(3, 0, V)
+        grad_store(3, 0)
+        grad_quant(3, 0)
+        scale_store_b()
+        code_store(3, 0)

@@ -20,12 +20,14 @@ GROUPS = 2
 CHUNK = 256
 CHUNKS = H // CHUNK
 BLOCKS = 4
-UNITS = CHUNKS * BLOCKS
+SPANS = [(0, 256), (256, 256), (512, 256), (768, 128), (896, 128)]
+SPAN_OF = [0, 0, 1, 1, 2, 2, 3, 4]
 LOSS_DIV = 32.0
 
 TR_BUFS = 2
 ACC_BUFS = 2
-WB = {"pool": 1, "act": 3, "dve": 2}
+ZB = 3
+WB = {"pool": 1, "act": 2, "dve": 1}
 
 FLOPS = 4 * 2 * N * D * H
 
@@ -52,7 +54,8 @@ def tile_gaussianrbmtwophasehiddenoffsetgrad_x1_kernel(tc, vpos, vneg, beta, u, 
         bl_rows = kept("bl_rows", [P, P], BF16)
         bl_col = kept("bl_col", [P, 16], F32)
         warm = kept("warm", [P, 1], F32)
-        u_raw = [kept("u_raw%d" % i, [P, GROUPS, PACK, CHUNK], BF16) for i in range(CHUNKS)]
+        u_raw = [kept("u_first", [P, GROUPS, PACK, CHUNK], BF16), kept("u_rest", [P, GROUPS, PACK, H - CHUNK], BF16)]
+        w_scaled = u_raw
         v_raw = [kept("v_raw%d" % i, [P, PACK, D], BF16) for i in range(BLOCKS)]
         vd_codes = [kept("vd_codes%d" % i, [P, GROUPS, KP], U32) for i in range(BLOCKS)]
         vd_scales = [kept("vd_scales%d" % i, [P, GROUPS, KP], U8) for i in range(BLOCKS)]
@@ -60,8 +63,8 @@ def tile_gaussianrbmtwophasehiddenoffsetgrad_x1_kernel(tc, vpos, vneg, beta, u, 
         vn_scales = [kept("vn_scales%d" % i, [P, GROUPS, KP], U8) for i in range(BLOCKS)]
         w_codes = [kept("w_codes%d" % i, [P, GROUPS, CHUNK], U32) for i in range(CHUNKS)]
         w_scales = [kept("w_scales%d" % i, [P, GROUPS, CHUNK], U8) for i in range(CHUNKS)]
-        g_codes = [kept("g_codes%d" % i, [P, H], U32) for i in range(BLOCKS)]
-        g_scales = [kept("g_scales%d" % i, [P, H], U8) for i in range(BLOCKS)]
+        g_codes = {(sp, ph): kept("g_codes%d%d" % (sp, ph), [P, GROUPS, SPANS[sp][1]], U32) for sp in range(5) for ph in range(2)}
+        g_scales = {(sp, ph): kept("g_scales%d%d" % (sp, ph), [P, GROUPS, SPANS[sp][1]], U8) for sp in range(5) for ph in range(2)}
         o_codes = kept("o_codes", [P, GROUPS, H], U32)
         o_scales = kept("o_scales", [P, GROUPS, H], U8)
         live = {}
@@ -71,10 +74,10 @@ def tile_gaussianrbmtwophasehiddenoffsetgrad_x1_kernel(tc, vpos, vneg, beta, u, 
             g = i % GROUPS
             return src[g * KP:(g + 1) * KP, :].rearrange("(p j) d -> p j d", j=PACK)
 
-        def load_u(hc):
-            cols = slice(hc * CHUNK, (hc + 1) * CHUNK)
+        def load_u(part):
+            cols = slice(0, CHUNK) if part == 0 else slice(CHUNK, H)
             for g in range(GROUPS):
-                nc.sync.dma_start(out=u_raw[hc][:, g, :, :], in_=u[g * KP:(g + 1) * KP, cols].rearrange("(p j) h -> p j h", j=PACK))
+                nc.sync.dma_start(out=u_raw[part][:, g, :, :], in_=u[g * KP:(g + 1) * KP, cols].rearrange("(p j) h -> p j h", j=PACK))
 
         def loads():
             nc.vector.memset(warm[:], 0.0)
@@ -90,11 +93,9 @@ def tile_gaussianrbmtwophasehiddenoffsetgrad_x1_kernel(tc, vpos, vneg, beta, u, 
             load_u(0)
             nc.sync.dma_start(out=v_raw[0][:, :, KP:D], in_=v_rows(0)[:, :, KP:D])
             nc.sync.dma_start(out=v_raw[1][:], in_=v_rows(1))
-            load_u(1)
             nc.sync.dma_start(out=v_raw[2][:], in_=v_rows(2))
             nc.sync.dma_start(out=v_raw[3][:], in_=v_rows(3))
-            load_u(2)
-            load_u(3)
+            load_u(1)
 
         def small_vector():
             flat_c = c_raw[:].rearrange("p g j -> p (g j)")
@@ -137,17 +138,15 @@ def tile_gaussianrbmtwophasehiddenoffsetgrad_x1_kernel(tc, vpos, vneg, beta, u, 
         def lane(copy):
             return "pool" if copy is pool_copy else "act" if copy is act_copy else "dve"
 
-        def w_scale(hc):
-            scaled = work.tile([P, GROUPS, PACK, CHUNK], BF16, name="w_scaled", bufs=1)
-            for g in range(GROUPS):
-                for j in range(PACK):
-                    k = PACK * g + j
-                    nc.vector.tensor_scalar(out=scaled[:, g, j, :], in0=u_raw[hc][:, g, j, :], scalar1=c_in[:, k:k + 1], scalar2=None, op0=ALU.mult)
-            live["w_scaled", hc] = scaled
+        def w_scale(part, g):
+            for j in range(PACK):
+                k = PACK * g + j
+                nc.vector.tensor_scalar(out=w_scaled[part][:, g, j, :], in0=u_raw[part][:, g, j, :], scalar1=c_in[:, k:k + 1], scalar2=None, op0=ALU.mult)
 
         def w_weave(hc, copy):
+            src = w_scaled[0][:] if hc == 0 else w_scaled[1][:, :, :, (hc - 1) * CHUNK:hc * CHUNK]
             woven = work.tile([P, GROUPS, CHUNK, PACK], BF16, name="woven_" + lane(copy), bufs=WB[lane(copy)], align_bytes=64)
-            copy(out=woven[:], in_=live["w_scaled", hc][:].rearrange("p g j h -> p g h j"))
+            copy(out=woven[:], in_=src.rearrange("p g j h -> p g h j"))
             live["w_woven", hc] = woven
 
         def w_quant(hc):
@@ -165,13 +164,14 @@ def tile_gaussianrbmtwophasehiddenoffsetgrad_x1_kernel(tc, vpos, vneg, beta, u, 
             live["vd_bank", i, g, half] = bank
 
         def vd_out(i, g, half):
-            if half == 0:
-                live["vd_woven", i, g] = work.tile([P, 2, P, 2, 2], F32, name="vd_woven", bufs=2, align_bytes=64)
-            nc.scalar.copy(out=live["vd_woven", i, g][:, half, :, :, :], in_=live["vd_bank", i, g, half][:].rearrange("p e w q -> p q e w"))
+            if ("vd_woven", i) not in live:
+                live["vd_woven", i] = work.tile([P, GROUPS, 2, P, 2, 2], F32, name="vd_woven", bufs=2, align_bytes=64)
+            nc.scalar.copy(out=live["vd_woven", i][:, g, half, :, :, :], in_=live["vd_bank", i, g, half][:].rearrange("p e w q -> p q e w"))
 
-        def vd_quant(i, g):
-            nc.vector.quantize_mx(out=vd_codes[i][:, g, :].bitcast(FP8X4), scales=vd_scales[i][:, g, :],
-                                  in_=live["vd_woven", i, g][:].rearrange("p a q e w -> p (a q e w)").bitcast(BF16))
+        def vd_quant(i, lo, hi):
+            nc.vector.quantize_mx(out=vd_codes[i][:, lo:hi, :].rearrange("p g n -> p (g n)").bitcast(FP8X4),
+                                  scales=vd_scales[i][:, lo:hi, :].rearrange("p g n -> p (g n)"),
+                                  in_=live["vd_woven", i][:, lo:hi].rearrange("p g a q e w -> p (g a q e w)").bitcast(BF16))
 
         def vn_weave(i, g, half, copy):
             if half == 0:
@@ -189,95 +189,94 @@ def tile_gaussianrbmtwophasehiddenoffsetgrad_x1_kernel(tc, vpos, vneg, beta, u, 
             nc.vector.quantize_mx(out=vn_codes[i][:, g, :].bitcast(FP8X4), scales=vn_scales[i][:, g, :],
                                   in_=live["vn_woven", i, g][:].rearrange("p t m j -> p (t m j)"))
 
-        def hidden_mm(un, a):
-            hc, i = divmod(un, BLOCKS)
+        def hidden_mm(ht, i):
+            hc, a = divmod(ht, 2)
             acc = psum.tile([P, KP], F32, name="acc", bufs=ACC_BUFS)
             cols = slice(a * P, (a + 1) * P)
             for g in range(GROUPS):
                 nc.tensor.matmul_mx(out=acc[:], lhsT=w_codes[hc][:, g, cols].bitcast(FP8X4), lhsT_scale=w_scales[hc][:, g, cols],
                                     rhs=vd_codes[i][:, g, :].bitcast(FP8X4), rhs_scale=vd_scales[i][:, g, :],
                                     start=(g == 0), stop=(g == GROUPS - 1))
-            live["acc", un, a] = acc
+            live["acc", ht, i] = acc
 
-        def hidden_beta(un, a):
-            z = work.tile([P, KP], F32, name="z", bufs=4)
-            nc.vector.tensor_tensor(out=z[:], in0=live["acc", un, a][:], in1=beta_row[:, un % BLOCKS, :], op=ALU.mult)
-            live["z", un, a] = z
-
-        def hidden_sigmoid(un, a):
-            hc, i = divmod(un, BLOCKS)
-            ht = 2 * hc + a
-            s = work.tile([P, KP], F32, name="s", bufs=4)
-            nc.scalar.activation(out=s[:], in_=live["z", un, a][:], func=ACT.Sigmoid, bias=bl_col[:, ht:ht + 1], scale=(-1.0 if i < GROUPS else 1.0))
-            live["s", un, a] = s
-
-        def beta_psum(i):
+        def hidden_beta(ht, i):
             ph, g = divmod(i, GROUPS)
-            return live["beta_bank", ph][:, 2 * g:2 * g + 2, :].rearrange("p k q -> p (k q)").bitcast(BF16)
+            if ("z", ht, ph) not in live:
+                live["z", ht, ph] = work.tile([P, GROUPS, KP], F32, name="z", bufs=ZB)
+            nc.vector.tensor_tensor(out=live["z", ht, ph][:, g, :], in0=live["acc", ht, i][:], in1=beta_row[:, i, :], op=ALU.mult)
 
-        def hidden_signal(un, a):
-            hc, i = divmod(un, BLOCKS)
-            ht = 2 * hc + a
-            gt = work.tile([P, KP], BF16, name="gt", bufs=4)
-            nc.vector.scalar_tensor_tensor(out=gt[:], in0=live["s", un, a][:], scalar=bl_col[:, 8 + ht:9 + ht], in1=beta_psum(i),
-                                           op0=ALU.subtract, op1=ALU.mult)
-            live["gt", un, a] = gt
+        def flat(tile, lo, hi):
+            return tile[:, lo:hi, :].rearrange("p g n -> p (g n)")
 
-        def g_turn(un):
-            bank = psum.tile([P, 2, 2, P], F32, name="tr", bufs=TR_BUFS)
-            for a in range(2):
-                words = live["gt", un, a][:].bitcast(F32)
+        def hidden_sigmoid(ht, ph, lo, hi):
+            if ("s", ht, ph) not in live:
+                live["s", ht, ph] = work.tile([P, GROUPS, KP], F32, name="s", bufs=ZB)
+            nc.scalar.activation(out=flat(live["s", ht, ph], lo, hi), in_=flat(live["z", ht, ph], lo, hi), func=ACT.Sigmoid,
+                                 bias=bl_col[:, ht:ht + 1], scale=(-1.0 if ph == 0 else 1.0))
+
+        def hidden_signal(ht, ph, lo, hi):
+            if ("gt", ht, ph) not in live:
+                live["gt", ht, ph] = work.tile([P, GROUPS, KP], BF16, name="gt", bufs=ZB)
+            beta_bf = live["beta_bank", ph][:, 2 * lo:2 * hi, :].rearrange("p k q -> p (k q)").bitcast(BF16)
+            nc.vector.scalar_tensor_tensor(out=flat(live["gt", ht, ph], lo, hi), in0=flat(live["s", ht, ph], lo, hi),
+                                           scalar=bl_col[:, 8 + ht:9 + ht], in1=beta_bf, op0=ALU.subtract, op1=ALU.mult)
+
+        def g_turn(ht, ph, lo, hi):
+            bank = psum.tile([P, hi - lo, 2, P], F32, name="tr", bufs=TR_BUFS)
+            for g in range(lo, hi):
+                words = live["gt", ht, ph][:, g, :].bitcast(F32)
                 for w in range(2):
-                    nc.tensor.transpose(bank[:, a, w, :], words[:, w * P:(w + 1) * P], ident_f[:])
-            live["g_bank", un] = bank
+                    nc.tensor.transpose(bank[:, g - lo, w, :], words[:, w * P:(w + 1) * P], ident_f[:])
+            live["g_bank", ht, ph, lo] = bank
 
-        def g_out(un):
-            woven = work.tile([P, 2, P, 2], F32, name="g_woven", bufs=3, align_bytes=64)
-            nc.scalar.copy(out=woven[:], in_=live["g_bank", un][:].rearrange("p a w h -> p a h w"))
-            live["g_woven", un] = woven
+        def g_out(ht, ph, lo, hi):
+            sp = SPAN_OF[ht]
+            first, width = SPANS[sp]
+            if ("g_woven", sp, ph) not in live:
+                live["g_woven", sp, ph] = work.tile([P, GROUPS, width, 2], F32, name="g_woven", bufs=3, align_bytes=64)
+            at = ht * P - first
+            nc.scalar.copy(out=live["g_woven", sp, ph][:, lo:hi, at:at + P, :], in_=live["g_bank", ht, ph, lo][:].rearrange("p g w h -> p g h w"))
 
-        def g_quant(un):
-            hc, i = divmod(un, BLOCKS)
-            cols = slice(hc * CHUNK, (hc + 1) * CHUNK)
-            nc.vector.quantize_mx(out=g_codes[i][:, cols].bitcast(FP8X4), scales=g_scales[i][:, cols],
-                                  in_=live["g_woven", un][:].rearrange("p a h w -> p (a h w)").bitcast(BF16))
+        def g_quant(sp, ph, lo, hi):
+            nc.vector.quantize_mx(out=flat(g_codes[sp, ph], lo, hi).bitcast(FP8X4), scales=flat(g_scales[sp, ph], lo, hi),
+                                  in_=live["g_woven", sp, ph][:, lo:hi].rearrange("p g h w -> p (g h w)").bitcast(BF16))
 
-        def grad_mm(hc, g, t, blocks=range(BLOCKS), tag="oacc"):
+        def grad_mm(sp, g, t, blocks=range(BLOCKS), tag="oacc"):
             if blocks[0] == 0:
-                live["oacc", hc, g, t] = psum.tile([P, CHUNK], F32, name=tag, bufs=2)
-            acc = live["oacc", hc, g, t]
+                live["oacc", sp, g, t] = psum.tile([P, SPANS[sp][1]], F32, name=tag, bufs=2)
+            acc = live["oacc", sp, g, t]
             rows = slice(t * P, (t + 1) * P)
-            cols = slice(hc * CHUNK, (hc + 1) * CHUNK)
             for i in blocks:
+                ph, ng = divmod(i, GROUPS)
                 nc.tensor.matmul_mx(out=acc[:], lhsT=vn_codes[i][:, g, rows].bitcast(FP8X4), lhsT_scale=vn_scales[i][:, g, rows],
-                                    rhs=g_codes[i][:, cols].bitcast(FP8X4), rhs_scale=g_scales[i][:, cols],
+                                    rhs=g_codes[sp, ph][:, ng, :].bitcast(FP8X4), rhs_scale=g_scales[sp, ph][:, ng, :],
                                     start=(i == 0), stop=(i == BLOCKS - 1))
 
-        def grad_out(hc, g, t, on="act"):
-            if t == 0:
-                live["res", hc, g] = work.tile([P, PACK, CHUNK], F32, name="res", bufs=3)
+        def grad_out(sp, g, t, on="act"):
+            if ("res", sp, g) not in live:
+                live["res", sp, g] = work.tile([P, PACK, SPANS[sp][1]], F32, name="res", bufs=3)
             k = PACK * g + t
             if on == "act":
-                nc.scalar.activation(out=live["res", hc, g][:, t, :], in_=live["oacc", hc, g, t][:], func=ACT.Copy, scale=c_out[:, k:k + 1])
+                nc.scalar.activation(out=live["res", sp, g][:, t, :], in_=live["oacc", sp, g, t][:], func=ACT.Copy, scale=c_out[:, k:k + 1])
             else:
-                nc.vector.tensor_scalar(out=live["res", hc, g][:, t, :], in0=live["oacc", hc, g, t][:], scalar1=c_out[:, k:k + 1], scalar2=None, op0=ALU.mult)
+                nc.vector.tensor_scalar(out=live["res", sp, g][:, t, :], in0=live["oacc", sp, g, t][:], scalar1=c_out[:, k:k + 1], scalar2=None, op0=ALU.mult)
 
-        def grad_store(hc, g):
-            cols = slice(hc * CHUNK, (hc + 1) * CHUNK)
-            nc.sync.dma_start(out=out_0[g * KP:(g + 1) * KP, cols].rearrange("(p t) m -> p t m", t=PACK), in_=live["res", hc, g][:])
+        def grad_store(sp, g):
+            cols = slice(SPANS[sp][0], SPANS[sp][0] + SPANS[sp][1])
+            nc.sync.dma_start(out=out_0[g * KP:(g + 1) * KP, cols].rearrange("(p t) m -> p t m", t=PACK), in_=live["res", sp, g][:])
 
-        def grad_weave(hc, g, copy):
-            woven = work.tile([P, CHUNK, PACK], BF16, name="res_woven_%s%d" % (lane(copy), g), bufs=1, align_bytes=64)
-            copy(out=woven[:], in_=live["res", hc, g][:].rearrange("p t m -> p m t"))
-            live["res_woven", hc, g] = woven
+        def grad_weave(sp, g, copy):
+            woven = work.tile([P, SPANS[sp][1], PACK], BF16, name="res_woven_%s%d" % (lane(copy), g), bufs=1, align_bytes=64)
+            copy(out=woven[:], in_=live["res", sp, g][:].rearrange("p t m -> p m t"))
+            live["res_woven", sp, g] = woven
 
-        def grad_quant(hc, g):
-            cols = slice(hc * CHUNK, (hc + 1) * CHUNK)
+        def grad_quant(sp, g):
+            cols = slice(SPANS[sp][0], SPANS[sp][0] + SPANS[sp][1])
             nc.vector.quantize_mx(out=o_codes[:, g, cols].bitcast(FP8X4), scales=o_scales[:, g, cols],
-                                  in_=live["res_woven", hc, g][:].rearrange("p m t -> p (m t)"))
+                                  in_=live["res_woven", sp, g][:].rearrange("p m t -> p (m t)"))
 
-        def code_store(hc, g):
-            cols = slice(hc * CHUNK, (hc + 1) * CHUNK)
+        def code_store(sp, g):
+            cols = slice(SPANS[sp][0], SPANS[sp][0] + SPANS[sp][1])
             nc.sync.dma_start(out=out_1[g, :, cols, :].rearrange("p m t -> p (m t)").bitcast(I32), in_=o_codes[:, g, cols].bitcast(I32))
 
         def scale_store(lo, hi, queues):
@@ -287,374 +286,359 @@ def tile_gaussianrbmtwophasehiddenoffsetgrad_x1_kernel(tc, vpos, vneg, beta, u, 
                     in_=o_scales[32 * q:32 * q + 4, :, lo:hi].bitcast(I32))
 
         def scale_store_a():
-            scale_store(0, 768, [nc.sync])
+            scale_store(0, 896, [nc.sync])
 
         def scale_store_b():
-            scale_store(768, 1024, [nc.sync, nc.scalar])
+            scale_store(896, 1024, [nc.sync, nc.scalar])
 
         G, A, V = pool_copy, act_copy, dve_copy
         loads()
-        small_vector()
-        vd_turn(0, 0, 0)
         vn_weave(0, 0, 0, V)
+        vd_turn(0, 0, 0)
+        vd_turn(0, 0, 1)
+        vd_out(0, 0, 0)
+        small_vector()
+        vd_out(0, 0, 1)
+        vn_quant(0, 0)
+        vd_quant(0, 0, 1)
+        w_scale(0, 1)
+        spread_bl()
+        vd_turn(0, 1, 0)
+        w_scale(0, 0)
+        bl_out()
+        vd_turn(0, 1, 1)
+        vd_out(0, 1, 0)
+        w_weave(0, V)
         spread_beta(0)
         spread_beta(1)
-        vd_out(0, 0, 0)
-        vd_turn(0, 0, 1)
-        beta_out(0)
-        w_scale(0)
-        beta_out(1)
-        w_weave(0, V)
-        vd_out(0, 0, 1)
-        vd_turn(0, 1, 0)
-        vn_weave(0, 1, 0, A)
-        vd_turn(0, 1, 1)
-        vd_quant(0, 0)
-        w_quant(0)
-        vd_out(0, 1, 0)
-        vn_quant(0, 0)
         vd_out(0, 1, 1)
-        vd_turn(1, 1, 0)
-        vn_weave(1, 0, 0, A)
-        vd_quant(0, 1)
-        vd_turn(1, 1, 1)
-        hidden_mm(0, 0)
-        w_scale(1)
-        vd_out(1, 1, 0)
-        hidden_mm(0, 1)
-        hidden_beta(0, 0)
-        vd_out(1, 1, 1)
         vd_turn(1, 0, 0)
-        w_weave(1, V)
-        vn_weave(1, 0, 1, A)
-        spread_bl()
-        hidden_beta(0, 1)
+        beta_out(1)
+        vd_quant(0, 1, 2)
+        vd_turn(1, 1, 0)
         vd_out(1, 0, 0)
-        w_quant(1)
-        bl_out()
-        vn_weave(1, 1, 0, A)
+        w_quant(0)
+        vd_out(1, 1, 0)
         vd_turn(1, 0, 1)
-        vn_quant(1, 0)
-        hidden_mm(4, 0)
-        vd_quant(1, 1)
-        hidden_sigmoid(0, 0)
-        hidden_mm(4, 1)
-        hidden_beta(4, 0)
+        vn_weave(0, 1, 0, V)
+        beta_out(0)
+        vd_turn(1, 1, 1)
         vd_out(1, 0, 1)
-        vd_turn(2, 1, 0)
-        hidden_signal(0, 0)
-        hidden_sigmoid(0, 1)
-        vd_turn(2, 1, 1)
-        vd_quant(1, 0)
-        hidden_sigmoid(4, 0)
-        hidden_beta(4, 1)
-        vd_out(2, 1, 0)
         hidden_mm(1, 0)
-        w_scale(2)
-        vd_out(2, 1, 1)
-        hidden_mm(1, 1)
-        vn_weave(0, 1, 1, A)
+        vd_out(1, 1, 1)
+        hidden_mm(0, 0)
         hidden_beta(1, 0)
-        vd_turn(2, 0, 0)
-        vd_quant(2, 1)
-        vd_turn(2, 0, 1)
-        hidden_signal(0, 1)
-        vd_out(2, 0, 0)
-        hidden_mm(5, 0)
-        hidden_beta(1, 1)
-        vd_out(2, 0, 1)
-        vd_turn(3, 0, 0)
-        hidden_signal(4, 0)
-        hidden_sigmoid(1, 0)
-        vd_quant(2, 0)
-        g_turn(0)
-        hidden_sigmoid(1, 1)
-        hidden_mm(5, 1)
-        hidden_beta(5, 0)
-        vd_out(3, 0, 0)
-        vn_quant(0, 1)
-        g_out(0)
-        vd_turn(3, 0, 1)
-        hidden_signal(1, 1)
-        hidden_sigmoid(4, 1)
-        hidden_mm(2, 1)
-        g_quant(0)
-        vn_weave(2, 1, 0, A)
-        hidden_signal(4, 1)
-        vd_turn(3, 1, 0)
-        hidden_beta(5, 1)
-        vd_out(3, 0, 1)
-        hidden_beta(2, 1)
-        hidden_mm(2, 0)
-        vd_out(3, 1, 0)
-        hidden_signal(1, 0)
-        hidden_mm(6, 0)
-        hidden_sigmoid(2, 1)
-        vd_quant(3, 0)
-        vd_turn(3, 1, 1)
-        hidden_sigmoid(5, 0)
-        hidden_beta(2, 0)
-        hidden_sigmoid(5, 1)
-        g_turn(4)
-        hidden_beta(6, 0)
-        vd_out(3, 1, 1)
-        hidden_signal(2, 1)
-        hidden_sigmoid(2, 0)
-        w_weave(2, V)
-        g_turn(1)
-        vn_weave(3, 1, 0, A)
-        hidden_mm(6, 1)
-        vd_quant(3, 1)
-        hidden_mm(3, 0)
-        g_out(4)
-        hidden_signal(5, 0)
-        vn_weave(1, 1, 1, A)
-        hidden_beta(6, 1)
-        hidden_signal(5, 1)
-        hidden_mm(3, 1)
-        hidden_sigmoid(6, 0)
-        hidden_beta(3, 0)
-        vn_weave(2, 1, 1, A)
-        hidden_beta(3, 1)
-        hidden_mm(7, 1)
-        hidden_signal(2, 0)
-        hidden_mm(7, 0)
-        vn_quant(1, 1)
-        hidden_sigmoid(3, 0)
-        g_turn(2)
-        hidden_beta(7, 1)
-        hidden_sigmoid(6, 1)
-        hidden_signal(3, 0)
-        hidden_sigmoid(3, 1)
-        w_quant(2)
-        g_out(1)
-        g_quant(4)
-        vn_weave(2, 0, 0, A)
-        hidden_beta(7, 0)
-        g_turn(5)
-        hidden_mm(8, 0)
-        w_scale(3)
-        hidden_mm(8, 1)
-        g_out(2)
-        hidden_signal(6, 0)
-        g_out(5)
-        g_quant(1)
-        g_quant(2)
-        vn_weave(3, 1, 1, A)
-        hidden_signal(3, 1)
-        g_turn(3)
-        hidden_signal(6, 1)
-        g_turn(6)
-        vn_quant(2, 1)
-        hidden_sigmoid(7, 0)
-        hidden_beta(8, 0)
-        hidden_sigmoid(7, 1)
-        hidden_beta(8, 1)
-        g_out(3)
-        hidden_mm(10, 1)
-        g_quant(5)
-        hidden_sigmoid(8, 0)
-        g_quant(3)
-        g_out(6)
-        vn_quant(3, 1)
-        grad_mm(0, 1, 0)
         vn_weave(3, 0, 0, A)
-        hidden_signal(7, 0)
-        grad_mm(0, 1, 1)
-        hidden_beta(10, 1)
-        hidden_mm(10, 0)
-        hidden_signal(7, 1)
-        hidden_sigmoid(8, 1)
-        g_turn(7)
-        hidden_signal(8, 0)
-        grad_out(0, 1, 0)
-        hidden_sigmoid(10, 1)
-        hidden_signal(8, 1)
-        grad_mm(0, 1, 3)
-        grad_out(0, 1, 1)
-        g_quant(6)
-        g_out(7)
-        hidden_beta(10, 0)
-        hidden_mm(9, 1)
-        vn_weave(2, 0, 1, A)
-        g_turn(8)
-        g_quant(7)
-        grad_mm(1, 1, 0)
-        hidden_beta(9, 1)
-        w_weave(3, V)
-        hidden_mm(9, 0)
-        grad_out(0, 1, 3)
-        grad_out(1, 1, 0)
-        grad_mm(0, 1, 2)
-        hidden_sigmoid(10, 0)
-        hidden_beta(9, 0)
-        hidden_mm(11, 1)
+        vd_turn(3, 0, 0)
+        vd_quant(1, 0, 2)
+        vd_turn(2, 0, 0)
+        hidden_beta(0, 0)
+        vd_out(3, 0, 0)
+        hidden_mm(0, 1)
+        vn_quant(0, 1)
+        vd_out(2, 0, 0)
+        hidden_mm(1, 1)
+        w_scale(1, 0)
         vn_weave(3, 0, 1, A)
-        w_quant(3)
-        grad_mm(1, 1, 3)
-        hidden_beta(11, 1)
-        hidden_mm(11, 0)
-        grad_out(0, 1, 2)
-        grad_out(1, 1, 3)
-        vn_quant(2, 0)
-        grad_mm(1, 1, 1)
-        grad_store(0, 1)
-        g_out(8)
+        vd_turn(2, 0, 1)
+        vd_turn(2, 1, 0)
+        hidden_beta(0, 1)
+        vd_out(2, 0, 1)
         vn_quant(3, 0)
-        hidden_mm(15, 0)
-        hidden_sigmoid(9, 1)
-        hidden_signal(10, 1)
+        vd_out(2, 1, 0)
+        vd_turn(2, 1, 1)
+        hidden_beta(1, 1)
+        vd_turn(3, 0, 1)
+        w_scale(1, 1)
+        vd_out(2, 1, 1)
+        vd_out(3, 0, 1)
+        vd_quant(2, 0, 2)
+        vd_turn(3, 1, 0)
+        hidden_sigmoid(1, 0, 0, 2)
+        vd_turn(3, 1, 1)
+        w_weave(1, G)
+        vd_out(3, 1, 0)
+        hidden_mm(0, 2)
+        hidden_signal(1, 0, 0, 2)
+        vd_out(3, 1, 1)
+        hidden_mm(1, 2)
+        vn_weave(1, 0, 0, A)
+        hidden_beta(0, 2)
+        hidden_beta(1, 2)
+        vn_weave(1, 0, 1, A)
+        vd_quant(3, 0, 2)
+        hidden_sigmoid(0, 0, 0, 2)
+        w_quant(1)
+        hidden_mm(0, 3)
+        vn_quant(1, 0)
+        hidden_mm(1, 3)
+        vn_weave(2, 1, 0, A)
+        vn_weave(2, 0, 0, G)
+        hidden_beta(0, 3)
+        hidden_beta(1, 3)
+        hidden_mm(2, 0)
+        hidden_signal(0, 0, 0, 2)
+        vn_weave(1, 1, 0, A)
+        hidden_mm(2, 1)
+        hidden_beta(2, 0)
+        hidden_sigmoid(0, 1, 0, 2)
+        hidden_beta(2, 1)
+        hidden_mm(2, 2)
+        vn_quant(2, 0)
+        hidden_sigmoid(1, 1, 0, 2)
+        hidden_mm(2, 3)
+        hidden_beta(2, 2)
+        g_turn(0, 0, 0, 2)
+        w_weave(2, G)
+        hidden_beta(2, 3)
+        hidden_mm(3, 0)
+        g_out(0, 0, 0, 2)
+        hidden_signal(0, 1, 0, 2)
+        g_turn(1, 0, 0, 2)
+        hidden_sigmoid(2, 0, 0, 2)
+        hidden_mm(3, 1)
+        hidden_beta(3, 0)
+        hidden_sigmoid(2, 1, 0, 2)
+        hidden_signal(1, 1, 0, 2)
+        hidden_mm(3, 2)
+        g_turn(0, 1, 0, 2)
+        g_out(1, 0, 0, 2)
+        hidden_beta(3, 1)
+        g_out(0, 1, 0, 2)
+        w_quant(2)
+        g_turn(1, 1, 0, 2)
+        hidden_signal(2, 0, 0, 2)
+        g_out(1, 1, 0, 2)
+        hidden_mm(4, 0)
+        vn_weave(3, 1, 0, G)
+        vn_weave(2, 1, 1, A)
+        hidden_beta(3, 2)
+        hidden_beta(4, 0)
+        hidden_mm(3, 3)
+        hidden_sigmoid(3, 0, 0, 2)
+        hidden_signal(2, 1, 0, 2)
+        hidden_mm(5, 0)
+        g_turn(2, 0, 0, 2)
+        vn_weave(1, 1, 1, A)
+        hidden_beta(3, 3)
+        g_turn(2, 1, 0, 2)
+        g_quant(0, 0, 0, 2)
+        hidden_mm(4, 1)
+        g_quant(0, 1, 0, 2)
+        hidden_sigmoid(3, 1, 0, 2)
         grad_mm(0, 0, 0)
-        grad_out(1, 1, 1)
-        hidden_beta(11, 0)
-        hidden_sigmoid(9, 0)
-        grad_mm(0, 0, 2)
-        hidden_beta(15, 0)
-        grad_out(0, 0, 0)
-        grad_weave(0, 1, A)
-        hidden_signal(9, 1)
-        grad_mm(1, 0, 0)
-        hidden_signal(10, 0)
-        hidden_mm(15, 1)
-        hidden_signal(9, 0)
-        grad_out(0, 0, 2)
-        hidden_mm(12, 1)
-        hidden_sigmoid(11, 1)
-        grad_mm(1, 0, 3)
-        grad_out(1, 0, 0)
-        hidden_beta(12, 1)
-        hidden_sigmoid(11, 0)
-        g_turn(10)
-        g_quant(8)
-        g_turn(9)
-        grad_out(1, 0, 3)
-        hidden_beta(15, 1)
-        grad_mm(1, 0, 2)
-        hidden_sigmoid(15, 0)
-        hidden_signal(11, 1)
-        g_out(9)
-        grad_mm(1, 1, 2)
-        hidden_signal(11, 0)
-        g_out(10)
-        hidden_mm(12, 0)
-        hidden_signal(15, 0)
-        grad_out(1, 1, 2)
-        hidden_mm(13, 1)
-        hidden_beta(12, 0)
-        grad_out(1, 0, 2)
-        g_turn(11)
-        grad_store(1, 1)
-        hidden_sigmoid(15, 1)
-        hidden_beta(13, 1)
-        grad_mm(0, 0, 3)
-        hidden_sigmoid(12, 1)
-        hidden_signal(15, 1)
+        hidden_beta(5, 0)
         grad_mm(0, 0, 1)
-        hidden_sigmoid(12, 0)
-        grad_weave(1, 1, V)
-        hidden_mm(13, 0)
-        grad_out(0, 0, 3)
-        g_out(11)
-        g_quant(10)
-        grad_mm(1, 0, 1)
-        hidden_beta(13, 0)
+        hidden_beta(4, 1)
+        grad_out(0, 0, 0)
+        hidden_mm(4, 2)
+        vn_quant(1, 1)
         grad_out(0, 0, 1)
-        g_turn(15)
-        hidden_sigmoid(13, 1)
-        hidden_signal(12, 1)
-        hidden_mm(14, 0)
-        grad_out(1, 0, 1)
-        g_quant(9)
-        grad_weave(0, 0, A)
-        g_quant(11)
-        hidden_mm(14, 1)
-        grad_store(1, 0)
+        grad_mm(0, 0, 2)
+        vn_quant(2, 1)
+        hidden_mm(5, 1)
+        vn_quant(3, 1)
+        grad_out(0, 0, 2)
+        grad_mm(0, 1, 0)
+        g_out(2, 0, 0, 2)
+        hidden_beta(4, 2)
+        w_weave(3, G)
+        grad_mm(0, 1, 1)
+        hidden_beta(5, 1)
+        grad_out(0, 1, 0)
+        hidden_mm(4, 3)
+        g_out(2, 1, 0, 2)
+        hidden_signal(3, 1, 0, 2)
+        grad_mm(0, 0, 3)
+        hidden_sigmoid(4, 0, 0, 2)
+        hidden_mm(5, 2)
+        hidden_signal(3, 0, 0, 2)
+        g_turn(3, 1, 0, 2)
+        grad_out(0, 1, 1)
+        grad_out(0, 0, 3)
+        hidden_beta(5, 2)
+        g_out(3, 1, 0, 2)
+        g_turn(3, 0, 0, 2)
         grad_store(0, 0)
-        hidden_signal(12, 0)
-        grad_mm(2, 0, 0)
-        hidden_beta(14, 1)
-        hidden_sigmoid(13, 0)
-        grad_mm(2, 0, 2)
-        hidden_beta(14, 0)
-        grad_out(2, 0, 0)
-        g_turn(12)
-        hidden_signal(13, 0)
-        g_out(15)
-        grad_mm(2, 0, 3)
-        hidden_signal(13, 1)
-        grad_out(2, 0, 2)
-        hidden_sigmoid(14, 1)
-        grad_mm(2, 0, 1)
-        grad_out(2, 0, 3)
-        hidden_signal(14, 1)
-        g_turn(13)
-        hidden_sigmoid(14, 0)
-        grad_mm(2, 1, 0)
-        g_quant(15)
-        grad_out(2, 0, 1)
-        hidden_signal(14, 0)
-        g_out(12)
-        grad_mm(2, 1, 1)
-        grad_quant(0, 0)
-        grad_out(2, 1, 0)
-        grad_weave(2, 0, V)
-        g_turn(14)
-        g_out(13)
-        code_store(0, 0)
-        grad_store(2, 0)
-        grad_mm(2, 1, 3)
-        grad_out(2, 1, 1)
+        hidden_beta(4, 3)
+        grad_mm(0, 1, 3)
+        g_out(3, 0, 0, 2)
+        hidden_signal(4, 0, 0, 2)
+        hidden_mm(5, 3)
+        hidden_sigmoid(5, 0, 0, 2)
+        grad_mm(0, 1, 2)
+        w_quant(3)
+        g_turn(4, 0, 0, 2)
+        grad_out(0, 1, 2)
+        g_quant(1, 0, 0, 2)
+        grad_out(0, 1, 3)
+        hidden_mm(6, 0)
+        g_quant(1, 1, 0, 2)
+        hidden_sigmoid(4, 1, 0, 2)
+        grad_store(0, 1)
+        grad_mm(1, 0, 0)
+        grad_weave(0, 1, G)
+        hidden_beta(5, 3)
+        grad_mm(1, 0, 3)
+        hidden_signal(5, 0, 0, 2)
+        grad_out(1, 0, 0)
+        hidden_mm(6, 1)
+        hidden_sigmoid(5, 1, 0, 2)
+        grad_weave(0, 0, G)
+        grad_mm(1, 0, 2)
+        hidden_beta(6, 0)
+        g_turn(5, 0, 0, 2)
+        hidden_beta(6, 1)
+        grad_out(1, 0, 3)
+        grad_out(1, 0, 2)
+        hidden_mm(7, 1)
+        hidden_signal(4, 1, 0, 2)
+        g_out(4, 0, 0, 2)
+        grad_mm(1, 0, 1)
+        g_out(5, 0, 0, 2)
+        grad_mm(1, 1, 0)
+        hidden_signal(5, 1, 0, 2)
+        grad_out(1, 0, 1)
+        hidden_mm(7, 0)
+        hidden_sigmoid(6, 0, 0, 2)
+        grad_store(1, 0)
+        grad_mm(1, 1, 3)
+        hidden_beta(7, 0)
+        g_turn(4, 1, 0, 2)
+        grad_out(1, 1, 0)
+        g_quant(2, 0, 0, 2)
+        g_turn(5, 1, 0, 2)
+        grad_out(1, 1, 3)
+        grad_mm(1, 1, 2)
+        g_out(4, 1, 0, 2)
+        hidden_beta(7, 1)
+        g_out(5, 1, 0, 2)
+        grad_mm(1, 1, 1)
         grad_quant(0, 1)
-        g_out(14)
-        g_quant(13)
+        grad_quant(0, 0)
+        grad_out(1, 1, 2)
+        hidden_mm(6, 2)
+        g_quant(2, 1, 0, 2)
+        grad_out(1, 1, 1)
+        hidden_mm(6, 3)
+        hidden_sigmoid(7, 0, 0, 2)
+        grad_weave(1, 0, G)
+        hidden_beta(6, 2)
+        grad_store(1, 1)
+        grad_mm(2, 1, 0)
+        hidden_beta(6, 3)
+        grad_mm(2, 0, 0)
+        grad_out(2, 1, 0)
+        hidden_signal(6, 0, 0, 2)
+        hidden_mm(7, 2)
+        hidden_sigmoid(6, 1, 0, 2)
+        grad_weave(1, 1, G)
         grad_mm(2, 1, 2)
-        code_store(0, 1)
-        g_quant(12)
-        grad_out(2, 1, 3)
-        g_quant(14)
-        grad_mm(3, 1, 0, range(3), "beta_bank")
+        hidden_beta(7, 2)
+        hidden_mm(7, 3)
+        grad_out(2, 0, 0)
+        hidden_signal(6, 1, 0, 2)
+        g_turn(6, 0, 0, 2)
+        hidden_sigmoid(7, 1, 0, 1)
+        grad_mm(2, 1, 3)
         grad_out(2, 1, 2)
-        grad_quant(1, 1)
-        grad_weave(1, 0, A)
-        grad_quant(2, 0)
-        grad_mm(3, 1, 0, range(3, 4))
-        grad_mm(3, 1, 2, range(3), "tr")
-        code_store(1, 1)
-        grad_weave(2, 1, V)
-        grad_store(2, 1)
-        code_store(2, 0)
-        grad_mm(3, 1, 3, range(3), "tr")
-        grad_mm(3, 1, 2, range(3, 4))
-        grad_mm(3, 1, 1, range(3), "beta_bank")
-        grad_quant(2, 1)
+        hidden_signal(7, 1, 0, 1)
+        g_out(6, 0, 0, 2)
+        g_turn(6, 1, 0, 2)
+        hidden_beta(7, 3)
+        grad_out(2, 1, 3)
+        grad_mm(2, 1, 1)
+        g_out(6, 1, 0, 2)
+        hidden_signal(7, 0, 0, 2)
+        grad_mm(2, 0, 3)
+        grad_out(2, 1, 1)
+        g_turn(7, 1, 0, 1)
+        grad_out(2, 0, 3)
+        grad_mm(2, 0, 1)
         grad_quant(1, 0)
-        grad_out(3, 1, 0, "act")
-        grad_mm(3, 1, 1, range(3, 4))
-        grad_mm(3, 1, 3, range(3, 4))
-        grad_out(3, 1, 2, "act")
-        grad_mm(3, 0, 3, range(3), "acc")
-        grad_out(3, 1, 1, "dve")
-        scale_store_a()
-        grad_out(3, 1, 3, "act")
-        grad_mm(3, 0, 3, range(3, 4))
-        grad_mm(3, 0, 0, range(3), "oacc")
+        hidden_sigmoid(7, 1, 1, 2)
+        g_quant(3, 0, 0, 2)
         code_store(1, 0)
-        grad_weave(3, 1, V)
-        grad_store(3, 1)
-        grad_mm(3, 0, 0, range(3, 4))
-        grad_mm(3, 0, 1, range(3), "oacc")
-        grad_out(3, 0, 0, "act")
-        grad_mm(3, 0, 2, range(3), "acc")
-        grad_out(3, 0, 3, "dve")
-        code_store(2, 1)
-        grad_quant(3, 1)
-        grad_mm(3, 0, 2, range(3, 4))
-        grad_mm(3, 0, 1, range(3, 4))
-        grad_out(3, 0, 2, "act")
-        code_store(3, 1)
-        grad_out(3, 0, 1, "dve")
-        grad_weave(3, 0, V)
+        grad_quant(1, 1)
+        grad_mm(2, 0, 2)
+        code_store(0, 0)
+        grad_store(2, 1)
+        code_store(0, 1)
+        grad_out(2, 0, 1)
+        g_quant(3, 1, 0, 2)
+        g_turn(7, 0, 0, 2)
+        grad_weave(2, 1, G)
+        hidden_signal(7, 1, 1, 2)
+        grad_out(2, 0, 2)
+        grad_mm(3, 0, 0)
+        g_out(7, 1, 0, 1)
+        grad_mm(3, 0, 2)
+        grad_store(2, 0)
+        grad_out(3, 0, 0)
+        g_turn(7, 1, 1, 2)
+        grad_out(3, 0, 2)
+        grad_weave(2, 0, G)
+        grad_mm(3, 0, 1)
+        g_out(7, 0, 0, 2)
+        grad_mm(3, 0, 3)
+        grad_out(3, 0, 1)
+        grad_out(3, 0, 3)
+        grad_mm(3, 1, 0)
+        g_out(7, 1, 1, 2)
+        g_quant(4, 0, 0, 2)
+        grad_mm(3, 1, 3)
         grad_store(3, 0)
+        code_store(1, 1)
+        grad_out(3, 1, 0)
+        grad_quant(2, 1)
+        grad_out(3, 1, 3)
+        g_quant(4, 1, 0, 1)
+        grad_mm(3, 1, 2)
+        grad_weave(3, 0, A)
+        grad_quant(2, 0)
+        grad_mm(3, 1, 1)
+        g_quant(4, 1, 1, 2)
+        grad_mm(4, 1, 0, range(3), "beta_bank")
+        code_store(2, 0)
+        grad_out(3, 1, 2)
+        code_store(2, 1)
+        grad_mm(4, 1, 1, range(3), "beta_bank")
+        grad_out(3, 1, 1)
         grad_quant(3, 0)
-        scale_store_b()
+        grad_mm(4, 1, 2, range(3), "tr")
+        grad_mm(4, 0, 3, range(3), "acc")
+        grad_weave(3, 1, V)
         code_store(3, 0)
+        grad_mm(4, 1, 0, range(3, 4))
+        grad_store(3, 1)
+        grad_mm(4, 1, 2, range(3, 4))
+        grad_mm(4, 1, 1, range(3, 4))
+        grad_mm(4, 0, 1, range(3), "oacc")
+        grad_out(4, 1, 0, "act")
+        grad_mm(4, 0, 1, range(3, 4))
+        grad_mm(4, 1, 3, range(3), "tr")
+        grad_out(4, 1, 2, "act")
+        grad_quant(3, 1)
+        grad_out(4, 1, 1, "dve")
+        grad_mm(4, 1, 3, range(3, 4))
+        grad_mm(4, 0, 2, range(3), "acc")
+        code_store(3, 1)
+        grad_mm(4, 0, 2, range(3, 4))
+        grad_out(4, 1, 3, "act")
+        scale_store_a()
+        grad_mm(4, 0, 3, range(3, 4))
+        grad_mm(4, 0, 0, range(3), "oacc")
+        grad_mm(4, 0, 0, range(3, 4))
+        grad_weave(4, 1, V)
+        grad_store(4, 1)
+        grad_out(4, 0, 0, "act")
+        grad_out(4, 0, 1, "dve")
+        grad_out(4, 0, 2, "act")
+        grad_out(4, 0, 3, "dve")
+        grad_weave(4, 0, V)
+        grad_store(4, 0)
+        grad_quant(4, 1)
+        grad_quant(4, 0)
+        code_store(4, 1)
+        scale_store_b()
+        code_store(4, 0)

@@ -27,7 +27,8 @@ LOSS_DIV = 32.0
 TR_BUFS = 2
 ACC_BUFS = 2
 ZB = 3
-WB = {"pool": 1, "act": 2, "dve": 1}
+GB = 2
+WB = {"pool": 1, "act": 2, "dve": 2}
 
 FLOPS = 4 * 2 * N * D * H
 
@@ -84,15 +85,16 @@ def tile_gaussianrbmtwophasehiddenoffsetgrad_x1_kernel(tc, vpos, vneg, beta, u, 
             nc.vector.memset(bl_rows[:], 0.0)
             make_identity(nc, ident_f[:])
             make_identity(nc, ident_b[:])
-            nc.sync.dma_start(out=v_raw[0][:, :, 0:KP], in_=v_rows(0)[:, :, 0:KP])
+            nc.sync.dma_start(out=v_raw[0][:, 0:2, 0:KP], in_=v_rows(0)[:, 0:2, 0:KP])
+            nc.sync.dma_start(out=v_raw[0][:, 2:4, 0:KP], in_=v_rows(0)[:, 2:4, 0:KP])
             nc.scalar.dma_start(out=c_raw[:], in_=c.rearrange("(g p j) -> p g j", g=GROUPS, j=PACK))
             nc.scalar.dma_start(out=beta_raw[:], in_=beta.rearrange("f (g p j) -> p (f g) j", g=GROUPS, j=PACK))
-            nc.scalar.dma_start(out=bl_rows[0:8, :], in_=b.rearrange("(r m) -> r m", m=P))
-            nc.scalar.dma_start(out=bl_rows[8:16, :], in_=lam.rearrange("(r m) -> r m", m=P))
-            nc.scalar.activation(out=warm[:], in_=warm[:], func=ACT.Sigmoid)
             load_u(0)
             nc.sync.dma_start(out=v_raw[0][:, :, KP:D], in_=v_rows(0)[:, :, KP:D])
             nc.sync.dma_start(out=v_raw[1][:], in_=v_rows(1))
+            nc.scalar.activation(out=warm[:], in_=warm[:], func=ACT.Sigmoid)
+            nc.sync.dma_start(out=bl_rows[0:8, :], in_=b.rearrange("(r m) -> r m", m=P))
+            nc.sync.dma_start(out=bl_rows[8:16, :], in_=lam.rearrange("(r m) -> r m", m=P))
             nc.sync.dma_start(out=v_raw[2][:], in_=v_rows(2))
             nc.sync.dma_start(out=v_raw[3][:], in_=v_rows(3))
             load_u(1)
@@ -233,7 +235,7 @@ def tile_gaussianrbmtwophasehiddenoffsetgrad_x1_kernel(tc, vpos, vneg, beta, u, 
             sp = SPAN_OF[ht]
             first, width = SPANS[sp]
             if ("g_woven", sp, ph) not in live:
-                live["g_woven", sp, ph] = work.tile([P, GROUPS, width, 2], F32, name="g_woven", bufs=3, align_bytes=64)
+                live["g_woven", sp, ph] = work.tile([P, GROUPS, width, 2], F32, name="g_woven", bufs=GB, align_bytes=64)
             at = ht * P - first
             nc.scalar.copy(out=live["g_woven", sp, ph][:, lo:hi, at:at + P, :], in_=live["g_bank", ht, ph, lo][:].rearrange("p g w h -> p g h w"))
 
@@ -293,352 +295,353 @@ def tile_gaussianrbmtwophasehiddenoffsetgrad_x1_kernel(tc, vpos, vneg, beta, u, 
 
         G, A, V = pool_copy, act_copy, dve_copy
         loads()
+        small_vector()
+        spread_beta(0)
         vn_weave(0, 0, 0, V)
         vd_turn(0, 0, 0)
+        beta_out(0)
         vd_turn(0, 0, 1)
         vd_out(0, 0, 0)
-        small_vector()
+        spread_beta(1)
+        w_scale(0, 1)
+        beta_out(1)
+        w_scale(0, 0)
         vd_out(0, 0, 1)
         vn_quant(0, 0)
-        vd_quant(0, 0, 1)
-        w_scale(0, 1)
-        spread_bl()
         vd_turn(0, 1, 0)
-        w_scale(0, 0)
-        bl_out()
+        w_weave(0, V)
         vd_turn(0, 1, 1)
         vd_out(0, 1, 0)
-        w_weave(0, V)
-        spread_beta(0)
-        spread_beta(1)
         vd_out(0, 1, 1)
-        vd_turn(1, 0, 0)
-        beta_out(1)
-        vd_quant(0, 1, 2)
-        vd_turn(1, 1, 0)
-        vd_out(1, 0, 0)
         w_quant(0)
-        vd_out(1, 1, 0)
+        vd_turn(1, 0, 0)
+        vd_quant(0, 0, 1)
         vd_turn(1, 0, 1)
-        vn_weave(0, 1, 0, V)
-        beta_out(0)
-        vd_turn(1, 1, 1)
+        vd_out(1, 0, 0)
+        vn_weave(1, 0, 0, V)
         vd_out(1, 0, 1)
-        hidden_mm(1, 0)
-        vd_out(1, 1, 1)
+        vd_turn(1, 1, 0)
+        vd_quant(0, 1, 2)
+        vd_turn(1, 1, 1)
+        vd_out(1, 1, 0)
         hidden_mm(0, 0)
-        hidden_beta(1, 0)
-        vn_weave(3, 0, 0, A)
-        vd_turn(3, 0, 0)
-        vd_quant(1, 0, 2)
+        vn_quant(1, 0)
+        vd_out(1, 1, 1)
         vd_turn(2, 0, 0)
         hidden_beta(0, 0)
-        vd_out(3, 0, 0)
-        hidden_mm(0, 1)
-        vn_quant(0, 1)
-        vd_out(2, 0, 0)
-        hidden_mm(1, 1)
-        w_scale(1, 0)
-        vn_weave(3, 0, 1, A)
         vd_turn(2, 0, 1)
-        vd_turn(2, 1, 0)
-        hidden_beta(0, 1)
+        vd_quant(1, 0, 2)
+        vd_out(2, 0, 0)
+        hidden_mm(1, 0)
         vd_out(2, 0, 1)
-        vn_quant(3, 0)
-        vd_out(2, 1, 0)
+        spread_bl()
+        hidden_beta(1, 0)
+        hidden_mm(0, 1)
+        bl_out()
+        vn_weave(3, 0, 0, A)
+        w_scale(1, 0)
+        vd_turn(2, 1, 0)
         vd_turn(2, 1, 1)
-        hidden_beta(1, 1)
-        vd_turn(3, 0, 1)
-        w_scale(1, 1)
+        hidden_beta(0, 1)
+        vd_out(2, 1, 0)
+        hidden_mm(1, 1)
         vd_out(2, 1, 1)
-        vd_out(3, 0, 1)
+        w_scale(1, 1)
+        vd_turn(3, 0, 0)
+        hidden_sigmoid(0, 0, 0, 2)
+        vd_turn(3, 0, 1)
         vd_quant(2, 0, 2)
-        vd_turn(3, 1, 0)
-        hidden_sigmoid(1, 0, 0, 2)
-        vd_turn(3, 1, 1)
+        vd_out(3, 0, 0)
+        vd_out(3, 0, 1)
         w_weave(1, G)
-        vd_out(3, 1, 0)
+        hidden_beta(1, 1)
         hidden_mm(0, 2)
+        hidden_signal(0, 0, 0, 2)
+        hidden_sigmoid(1, 0, 0, 2)
+        vd_turn(3, 1, 0)
+        vd_turn(3, 1, 1)
+        hidden_beta(0, 2)
+        vd_out(3, 1, 0)
+        hidden_mm(1, 2)
         hidden_signal(1, 0, 0, 2)
         vd_out(3, 1, 1)
-        hidden_mm(1, 2)
-        vn_weave(1, 0, 0, A)
-        hidden_beta(0, 2)
+        g_turn(0, 0, 0, 2)
+        vn_weave(3, 0, 1, A)
         hidden_beta(1, 2)
-        vn_weave(1, 0, 1, A)
         vd_quant(3, 0, 2)
-        hidden_sigmoid(0, 0, 0, 2)
+        g_out(0, 0, 0, 2)
+        vn_weave(2, 1, 0, A)
         w_quant(1)
         hidden_mm(0, 3)
-        vn_quant(1, 0)
-        hidden_mm(1, 3)
-        vn_weave(2, 1, 0, A)
-        vn_weave(2, 0, 0, G)
-        hidden_beta(0, 3)
-        hidden_beta(1, 3)
+        vn_quant(3, 0)
         hidden_mm(2, 0)
-        hidden_signal(0, 0, 0, 2)
-        vn_weave(1, 1, 0, A)
-        hidden_mm(2, 1)
-        hidden_beta(2, 0)
-        hidden_sigmoid(0, 1, 0, 2)
-        hidden_beta(2, 1)
-        hidden_mm(2, 2)
-        vn_quant(2, 0)
-        hidden_sigmoid(1, 1, 0, 2)
-        hidden_mm(2, 3)
-        hidden_beta(2, 2)
-        g_turn(0, 0, 0, 2)
         w_weave(2, G)
+        hidden_beta(0, 3)
+        vn_weave(2, 1, 1, A)
+        hidden_beta(2, 0)
+        hidden_mm(1, 3)
+        hidden_sigmoid(0, 1, 0, 2)
+        hidden_mm(2, 1)
+        hidden_beta(1, 3)
+        g_turn(1, 0, 0, 2)
+        hidden_beta(2, 1)
+        hidden_sigmoid(1, 1, 0, 2)
+        hidden_mm(2, 2)
+        hidden_signal(0, 1, 0, 2)
+        hidden_mm(3, 2)
+        vn_weave(2, 0, 0, A)
+        hidden_beta(2, 2)
+        g_turn(0, 1, 0, 2)
+        hidden_beta(3, 2)
+        hidden_mm(3, 3)
+        hidden_sigmoid(2, 0, 0, 2)
+        vn_quant(2, 1)
+        hidden_mm(2, 3)
+        w_quant(2)
+        vn_weave(1, 1, 0, A)
+        hidden_beta(3, 3)
+        w_weave(3, G)
         hidden_beta(2, 3)
         hidden_mm(3, 0)
-        g_out(0, 0, 0, 2)
-        hidden_signal(0, 1, 0, 2)
-        g_turn(1, 0, 0, 2)
-        hidden_sigmoid(2, 0, 0, 2)
-        hidden_mm(3, 1)
-        hidden_beta(3, 0)
-        hidden_sigmoid(2, 1, 0, 2)
-        hidden_signal(1, 1, 0, 2)
-        hidden_mm(3, 2)
-        g_turn(0, 1, 0, 2)
-        g_out(1, 0, 0, 2)
-        hidden_beta(3, 1)
         g_out(0, 1, 0, 2)
-        w_quant(2)
-        g_turn(1, 1, 0, 2)
+        hidden_signal(1, 1, 0, 2)
+        hidden_mm(3, 1)
+        g_out(1, 0, 0, 2)
         hidden_signal(2, 0, 0, 2)
+        vn_weave(2, 0, 1, A)
+        g_turn(1, 1, 0, 2)
+        hidden_beta(3, 0)
         g_out(1, 1, 0, 2)
-        hidden_mm(4, 0)
-        vn_weave(3, 1, 0, G)
-        vn_weave(2, 1, 1, A)
-        hidden_beta(3, 2)
-        hidden_beta(4, 0)
-        hidden_mm(3, 3)
-        hidden_sigmoid(3, 0, 0, 2)
-        hidden_signal(2, 1, 0, 2)
-        hidden_mm(5, 0)
-        g_turn(2, 0, 0, 2)
+        hidden_beta(3, 1)
         vn_weave(1, 1, 1, A)
-        hidden_beta(3, 3)
-        g_turn(2, 1, 0, 2)
+        hidden_mm(5, 0)
         g_quant(0, 0, 0, 2)
-        hidden_mm(4, 1)
+        hidden_mm(5, 1)
         g_quant(0, 1, 0, 2)
         hidden_sigmoid(3, 1, 0, 2)
+        vn_quant(2, 0)
         grad_mm(0, 0, 0)
+        vn_weave(0, 1, 0, V)
+        hidden_sigmoid(2, 1, 0, 2)
+        grad_mm(0, 0, 3)
+        w_quant(3)
+        grad_out(0, 0, 0)
+        grad_out(0, 0, 3)
+        vn_quant(1, 1)
+        grad_mm(0, 0, 2)
+        vn_weave(3, 1, 0, A)
         hidden_beta(5, 0)
         grad_mm(0, 0, 1)
-        hidden_beta(4, 1)
-        grad_out(0, 0, 0)
-        hidden_mm(4, 2)
-        vn_quant(1, 1)
-        grad_out(0, 0, 1)
-        grad_mm(0, 0, 2)
-        vn_quant(2, 1)
-        hidden_mm(5, 1)
-        vn_quant(3, 1)
-        grad_out(0, 0, 2)
-        grad_mm(0, 1, 0)
-        g_out(2, 0, 0, 2)
-        hidden_beta(4, 2)
-        w_weave(3, G)
-        grad_mm(0, 1, 1)
         hidden_beta(5, 1)
-        grad_out(0, 1, 0)
-        hidden_mm(4, 3)
-        g_out(2, 1, 0, 2)
+        hidden_mm(4, 0)
+        vn_weave(3, 1, 1, A)
+        hidden_signal(2, 1, 0, 2)
+        hidden_mm(4, 1)
+        g_turn(2, 0, 0, 2)
+        grad_out(0, 0, 2)
+        hidden_beta(4, 0)
+        g_turn(2, 1, 0, 2)
+        hidden_sigmoid(3, 0, 0, 2)
+        vn_quant(0, 1)
+        hidden_mm(4, 2)
+        hidden_beta(4, 1)
+        g_out(2, 0, 0, 2)
+        vn_quant(3, 1)
+        grad_mm(0, 1, 0)
+        grad_out(0, 0, 1)
         hidden_signal(3, 1, 0, 2)
-        grad_mm(0, 0, 3)
-        hidden_sigmoid(4, 0, 0, 2)
+        grad_weave(0, 0, G)
+        grad_store(0, 0)
+        hidden_mm(4, 3)
+        grad_out(0, 1, 0)
+        grad_mm(0, 1, 2)
+        hidden_beta(4, 2)
+        hidden_sigmoid(5, 0, 0, 2)
+        grad_mm(0, 1, 1)
+        hidden_beta(4, 3)
         hidden_mm(5, 2)
         hidden_signal(3, 0, 0, 2)
+        g_out(2, 1, 0, 2)
         g_turn(3, 1, 0, 2)
-        grad_out(0, 1, 1)
-        grad_out(0, 0, 3)
-        hidden_beta(5, 2)
-        g_out(3, 1, 0, 2)
-        g_turn(3, 0, 0, 2)
-        grad_store(0, 0)
-        hidden_beta(4, 3)
-        grad_mm(0, 1, 3)
-        g_out(3, 0, 0, 2)
-        hidden_signal(4, 0, 0, 2)
-        hidden_mm(5, 3)
-        hidden_sigmoid(5, 0, 0, 2)
-        grad_mm(0, 1, 2)
-        w_quant(3)
-        g_turn(4, 0, 0, 2)
         grad_out(0, 1, 2)
-        g_quant(1, 0, 0, 2)
-        grad_out(0, 1, 3)
+        hidden_beta(5, 2)
+        hidden_sigmoid(4, 0, 0, 2)
+        g_turn(3, 0, 0, 2)
+        hidden_signal(5, 0, 0, 2)
         hidden_mm(6, 0)
+        g_out(3, 0, 0, 2)
+        grad_mm(0, 1, 3)
+        hidden_beta(6, 0)
+        g_out(3, 1, 0, 2)
+        hidden_mm(6, 1)
+        g_quant(1, 0, 0, 2)
+        grad_out(0, 1, 1)
+        hidden_mm(5, 3)
+        grad_out(0, 1, 3)
         g_quant(1, 1, 0, 2)
         hidden_sigmoid(4, 1, 0, 2)
-        grad_store(0, 1)
         grad_mm(1, 0, 0)
+        grad_store(0, 1)
         grad_weave(0, 1, G)
-        hidden_beta(5, 3)
-        grad_mm(1, 0, 3)
-        hidden_signal(5, 0, 0, 2)
-        grad_out(1, 0, 0)
-        hidden_mm(6, 1)
-        hidden_sigmoid(5, 1, 0, 2)
-        grad_weave(0, 0, G)
-        grad_mm(1, 0, 2)
-        hidden_beta(6, 0)
-        g_turn(5, 0, 0, 2)
         hidden_beta(6, 1)
+        grad_mm(1, 0, 1)
+        hidden_beta(5, 3)
+        grad_out(1, 0, 0)
+        hidden_mm(6, 2)
+        hidden_signal(4, 0, 0, 2)
+        grad_out(1, 0, 1)
+        grad_mm(1, 0, 3)
+        hidden_sigmoid(5, 1, 0, 2)
+        grad_mm(1, 0, 2)
+        hidden_signal(4, 1, 0, 2)
+        g_turn(4, 0, 0, 2)
         grad_out(1, 0, 3)
         grad_out(1, 0, 2)
-        hidden_mm(7, 1)
-        hidden_signal(4, 1, 0, 2)
-        g_out(4, 0, 0, 2)
-        grad_mm(1, 0, 1)
-        g_out(5, 0, 0, 2)
+        g_turn(5, 0, 0, 2)
+        hidden_beta(6, 2)
         grad_mm(1, 1, 0)
-        hidden_signal(5, 1, 0, 2)
-        grad_out(1, 0, 1)
-        hidden_mm(7, 0)
-        hidden_sigmoid(6, 0, 0, 2)
+        g_out(4, 0, 0, 2)
         grad_store(1, 0)
-        grad_mm(1, 1, 3)
-        hidden_beta(7, 0)
-        g_turn(4, 1, 0, 2)
-        grad_out(1, 1, 0)
-        g_quant(2, 0, 0, 2)
-        g_turn(5, 1, 0, 2)
-        grad_out(1, 1, 3)
+        hidden_signal(5, 1, 0, 2)
+        g_out(5, 0, 0, 2)
         grad_mm(1, 1, 2)
-        g_out(4, 1, 0, 2)
-        hidden_beta(7, 1)
-        g_out(5, 1, 0, 2)
-        grad_mm(1, 1, 1)
-        grad_quant(0, 1)
-        grad_quant(0, 0)
+        grad_out(1, 1, 0)
+        hidden_mm(6, 3)
         grad_out(1, 1, 2)
-        hidden_mm(6, 2)
+        grad_quant(0, 0)
+        g_turn(4, 1, 0, 2)
+        g_quant(2, 0, 0, 2)
+        hidden_sigmoid(6, 0, 0, 2)
+        g_turn(5, 1, 0, 2)
+        grad_weave(1, 0, G)
+        hidden_beta(6, 3)
+        grad_mm(1, 1, 3)
+        g_out(4, 1, 0, 2)
+        grad_mm(1, 1, 1)
+        hidden_signal(6, 0, 0, 2)
+        g_out(5, 1, 0, 2)
+        hidden_mm(7, 0)
+        grad_out(1, 1, 3)
+        hidden_mm(7, 1)
         g_quant(2, 1, 0, 2)
         grad_out(1, 1, 1)
-        hidden_mm(6, 3)
-        hidden_sigmoid(7, 0, 0, 2)
-        grad_weave(1, 0, G)
-        hidden_beta(6, 2)
-        grad_store(1, 1)
         grad_mm(2, 1, 0)
-        hidden_beta(6, 3)
-        grad_mm(2, 0, 0)
-        grad_out(2, 1, 0)
-        hidden_signal(6, 0, 0, 2)
-        hidden_mm(7, 2)
         hidden_sigmoid(6, 1, 0, 2)
-        grad_weave(1, 1, G)
-        grad_mm(2, 1, 2)
-        hidden_beta(7, 2)
-        hidden_mm(7, 3)
-        grad_out(2, 0, 0)
-        hidden_signal(6, 1, 0, 2)
-        g_turn(6, 0, 0, 2)
-        hidden_sigmoid(7, 1, 0, 1)
+        hidden_beta(7, 0)
+        grad_store(1, 1)
         grad_mm(2, 1, 3)
-        grad_out(2, 1, 2)
-        hidden_signal(7, 1, 0, 1)
-        g_out(6, 0, 0, 2)
-        g_turn(6, 1, 0, 2)
-        hidden_beta(7, 3)
+        hidden_beta(7, 1)
+        grad_out(2, 1, 0)
+        hidden_mm(7, 2)
+        grad_quant(0, 1)
         grad_out(2, 1, 3)
-        grad_mm(2, 1, 1)
-        g_out(6, 1, 0, 2)
-        hidden_signal(7, 0, 0, 2)
-        grad_mm(2, 0, 3)
-        grad_out(2, 1, 1)
-        g_turn(7, 1, 0, 1)
-        grad_out(2, 0, 3)
-        grad_mm(2, 0, 1)
-        grad_quant(1, 0)
-        hidden_sigmoid(7, 1, 1, 2)
-        g_quant(3, 0, 0, 2)
-        code_store(1, 0)
-        grad_quant(1, 1)
-        grad_mm(2, 0, 2)
-        code_store(0, 0)
-        grad_store(2, 1)
+        hidden_signal(6, 1, 0, 2)
+        grad_mm(2, 1, 2)
+        hidden_sigmoid(7, 0, 0, 2)
+        grad_weave(1, 1, G)
         code_store(0, 1)
-        grad_out(2, 0, 1)
+        grad_mm(2, 0, 0)
+        hidden_beta(7, 2)
+        g_turn(6, 0, 0, 2)
+        grad_out(2, 1, 2)
+        grad_out(2, 0, 0)
+        g_turn(6, 1, 0, 2)
+        grad_mm(2, 1, 1)
+        grad_quant(1, 1)
+        g_out(6, 0, 0, 2)
+        grad_quant(1, 0)
+        g_out(6, 1, 0, 2)
+        grad_mm(2, 0, 2)
+        g_quant(3, 0, 0, 2)
+        grad_out(2, 1, 1)
+        hidden_mm(7, 3)
         g_quant(3, 1, 0, 2)
-        g_turn(7, 0, 0, 2)
-        grad_weave(2, 1, G)
-        hidden_signal(7, 1, 1, 2)
         grad_out(2, 0, 2)
+        hidden_signal(7, 0, 0, 2)
         grad_mm(3, 0, 0)
-        g_out(7, 1, 0, 1)
-        grad_mm(3, 0, 2)
-        grad_store(2, 0)
+        grad_weave(2, 1, G)
+        grad_store(2, 1)
+        hidden_sigmoid(7, 1, 0, 1)
+        grad_mm(2, 0, 1)
         grad_out(3, 0, 0)
-        g_turn(7, 1, 1, 2)
-        grad_out(3, 0, 2)
-        grad_weave(2, 0, G)
-        grad_mm(3, 0, 1)
-        g_out(7, 0, 0, 2)
-        grad_mm(3, 0, 3)
-        grad_out(3, 0, 1)
-        grad_out(3, 0, 3)
-        grad_mm(3, 1, 0)
-        g_out(7, 1, 1, 2)
-        g_quant(4, 0, 0, 2)
-        grad_mm(3, 1, 3)
-        grad_store(3, 0)
-        code_store(1, 1)
-        grad_out(3, 1, 0)
+        hidden_beta(7, 3)
+        grad_mm(2, 0, 3)
+        grad_out(2, 0, 1)
         grad_quant(2, 1)
-        grad_out(3, 1, 3)
-        g_quant(4, 1, 0, 1)
-        grad_mm(3, 1, 2)
-        grad_weave(3, 0, A)
-        grad_quant(2, 0)
-        grad_mm(3, 1, 1)
-        g_quant(4, 1, 1, 2)
-        grad_mm(4, 1, 0, range(3), "beta_bank")
-        code_store(2, 0)
-        grad_out(3, 1, 2)
+        grad_mm(3, 0, 3)
+        grad_out(2, 0, 3)
+        hidden_signal(7, 1, 0, 1)
+        g_turn(7, 0, 0, 2)
         code_store(2, 1)
+        grad_out(3, 0, 3)
+        code_store(1, 1)
+        grad_mm(3, 0, 2)
+        grad_weave(2, 0, G)
+        grad_store(2, 0)
+        hidden_sigmoid(7, 1, 1, 2)
+        code_store(0, 0)
+        code_store(1, 0)
+        grad_mm(3, 0, 1)
+        grad_out(3, 0, 2)
+        hidden_signal(7, 1, 1, 2)
+        grad_out(3, 0, 1)
+        grad_mm(3, 1, 0)
+        g_out(7, 0, 0, 2)
+        grad_mm(3, 1, 2)
+        grad_store(3, 0)
+        grad_weave(3, 0, V)
+        grad_out(3, 1, 0)
+        g_turn(7, 1, 0, 1)
+        grad_quant(2, 0)
+        grad_out(3, 1, 2)
+        g_turn(7, 1, 1, 2)
+        g_quant(4, 0, 0, 2)
+        grad_mm(3, 1, 1)
+        g_out(7, 1, 0, 1)
+        code_store(2, 0)
+        grad_mm(3, 1, 3)
+        g_out(7, 1, 1, 2)
+        g_quant(4, 1, 0, 1)
         grad_mm(4, 1, 1, range(3), "beta_bank")
         grad_out(3, 1, 1)
         grad_quant(3, 0)
+        grad_out(3, 1, 3)
+        g_quant(4, 1, 1, 2)
         grad_mm(4, 1, 2, range(3), "tr")
-        grad_mm(4, 0, 3, range(3), "acc")
-        grad_weave(3, 1, V)
         code_store(3, 0)
-        grad_mm(4, 1, 0, range(3, 4))
+        grad_weave(3, 1, V)
         grad_store(3, 1)
+        grad_mm(4, 1, 0, range(3), "beta_bank")
+        grad_mm(4, 1, 0, range(3, 4))
         grad_mm(4, 1, 2, range(3, 4))
-        grad_mm(4, 1, 1, range(3, 4))
-        grad_mm(4, 0, 1, range(3), "oacc")
-        grad_out(4, 1, 0, "act")
-        grad_mm(4, 0, 1, range(3, 4))
         grad_mm(4, 1, 3, range(3), "tr")
-        grad_out(4, 1, 2, "act")
-        grad_quant(3, 1)
-        grad_out(4, 1, 1, "dve")
+        grad_out(4, 1, 0, "act")
         grad_mm(4, 1, 3, range(3, 4))
-        grad_mm(4, 0, 2, range(3), "acc")
-        code_store(3, 1)
-        grad_mm(4, 0, 2, range(3, 4))
-        grad_out(4, 1, 3, "act")
-        scale_store_a()
+        grad_quant(3, 1)
+        grad_mm(4, 1, 1, range(3, 4))
+        grad_mm(4, 0, 3, range(3), "acc")
+        grad_out(4, 1, 2, "act")
         grad_mm(4, 0, 3, range(3, 4))
+        grad_out(4, 1, 3, "act")
+        grad_out(4, 1, 1, "dve")
+        grad_mm(4, 0, 2, range(3), "acc")
+        scale_store_a()
         grad_mm(4, 0, 0, range(3), "oacc")
-        grad_mm(4, 0, 0, range(3, 4))
+        code_store(3, 1)
         grad_weave(4, 1, V)
+        grad_mm(4, 0, 0, range(3, 4))
         grad_store(4, 1)
+        grad_mm(4, 0, 2, range(3, 4))
+        grad_mm(4, 0, 1, range(3), "oacc")
         grad_out(4, 0, 0, "act")
-        grad_out(4, 0, 1, "dve")
-        grad_out(4, 0, 2, "act")
         grad_out(4, 0, 3, "dve")
+        grad_mm(4, 0, 1, range(3, 4))
+        grad_out(4, 0, 2, "act")
+        grad_quant(4, 1)
+        grad_out(4, 0, 1, "dve")
+        code_store(4, 1)
         grad_weave(4, 0, V)
         grad_store(4, 0)
-        grad_quant(4, 1)
         grad_quant(4, 0)
-        code_store(4, 1)
-        scale_store_b()
         code_store(4, 0)
+        scale_store_b()

@@ -29,6 +29,7 @@ ACC_BUFS = 2
 ZB = 3
 GB = 2
 WB = {"pool": 1, "act": 2, "dve": 2}
+PB = {"oacc0": 1, "oacc1": 1, "acc": 2, "tr": 2, "beta_bank": 2}
 
 FLOPS = 4 * 2 * N * D * H
 
@@ -158,7 +159,8 @@ def tile_gaussianrbmtwophasehiddenoffsetgrad_x1_kernel(tc, vpos, vneg, beta, u, 
                 in_=live["w_woven", hc][:].rearrange("p g h j -> p (g h j)"))
 
         def vd_turn(i, g, half):
-            bank = psum.tile([P, 2, 2, P], F32, name="tr", bufs=TR_BUFS)
+            tag = "oacc1" if (4 * i + 2 * g + half) % 3 == 2 else "tr"
+            bank = psum.tile([P, 2, 2, P], F32, name=tag, bufs=PB[tag])
             for e in range(2):
                 words = v_raw[i][:, 2 * half + e, :].bitcast(F32)
                 for w in range(2):
@@ -190,6 +192,12 @@ def tile_gaussianrbmtwophasehiddenoffsetgrad_x1_kernel(tc, vpos, vneg, beta, u, 
         def vn_quant(i, g):
             nc.vector.quantize_mx(out=vn_codes[i][:, g, :].bitcast(FP8X4), scales=vn_scales[i][:, g, :],
                                   in_=live["vn_woven", i, g][:].rearrange("p t m j -> p (t m j)"))
+
+        def keep_clock(k):
+            if "idle_bank" not in live:
+                live["idle_bank"] = psum.tile([P, KP], F32, name="oacc0", bufs=1)
+            nc.tensor.matmul_mx(out=live["idle_bank"][:], lhsT=vn_codes[0][:, 0, 0:P].bitcast(FP8X4), lhsT_scale=vn_scales[0][:, 0, 0:P],
+                                rhs=vn_codes[0][:, 0, :].bitcast(FP8X4), rhs_scale=vn_scales[0][:, 0, :], start=True, stop=True)
 
         def hidden_mm(ht, i):
             hc, a = divmod(ht, 2)
@@ -243,9 +251,9 @@ def tile_gaussianrbmtwophasehiddenoffsetgrad_x1_kernel(tc, vpos, vneg, beta, u, 
             nc.vector.quantize_mx(out=flat(g_codes[sp, ph], lo, hi).bitcast(FP8X4), scales=flat(g_scales[sp, ph], lo, hi),
                                   in_=live["g_woven", sp, ph][:, lo:hi].rearrange("p g h w -> p (g h w)").bitcast(BF16))
 
-        def grad_mm(sp, g, t, blocks=range(BLOCKS), tag="oacc"):
+        def grad_mm(sp, g, t, blocks=range(BLOCKS), tag=None):
             if blocks[0] == 0:
-                live["oacc", sp, g, t] = psum.tile([P, SPANS[sp][1]], F32, name=tag, bufs=2)
+                live["oacc", sp, g, t] = psum.tile([P, SPANS[sp][1]], F32, name=tag or "oacc%d" % (t % 2), bufs=PB[tag or "oacc0"])
             acc = live["oacc", sp, g, t]
             rows = slice(t * P, (t + 1) * P)
             for i in blocks:
@@ -296,352 +304,377 @@ def tile_gaussianrbmtwophasehiddenoffsetgrad_x1_kernel(tc, vpos, vneg, beta, u, 
         G, A, V = pool_copy, act_copy, dve_copy
         loads()
         small_vector()
-        spread_beta(0)
-        vn_weave(0, 0, 0, V)
         vd_turn(0, 0, 0)
-        beta_out(0)
+        vn_weave(0, 0, 0, V)
         vd_turn(0, 0, 1)
         vd_out(0, 0, 0)
         spread_beta(1)
-        w_scale(0, 1)
-        beta_out(1)
-        w_scale(0, 0)
-        vd_out(0, 0, 1)
         vn_quant(0, 0)
-        vd_turn(0, 1, 0)
+        vd_out(0, 0, 1)
+        w_scale(0, 0)
+        keep_clock(0)
+        beta_out(1)
+        w_scale(0, 1)
+        keep_clock(1)
+        vd_quant(0, 0, 1)
+        keep_clock(2)
         w_weave(0, V)
+        vd_turn(0, 1, 0)
+        vn_weave(1, 0, 0, V)
         vd_turn(0, 1, 1)
         vd_out(0, 1, 0)
-        vd_out(0, 1, 1)
-        w_quant(0)
         vd_turn(1, 0, 0)
-        vd_quant(0, 0, 1)
+        w_quant(0)
+        vd_out(0, 1, 1)
+        spread_beta(0)
         vd_turn(1, 0, 1)
         vd_out(1, 0, 0)
-        vn_weave(1, 0, 0, V)
-        vd_out(1, 0, 1)
-        vd_turn(1, 1, 0)
         vd_quant(0, 1, 2)
+        vd_turn(1, 1, 0)
+        beta_out(0)
+        vn_weave(0, 1, 0, V)
+        vd_out(1, 0, 1)
         vd_turn(1, 1, 1)
         vd_out(1, 1, 0)
-        hidden_mm(0, 0)
         vn_quant(1, 0)
-        vd_out(1, 1, 1)
-        vd_turn(2, 0, 0)
-        hidden_beta(0, 0)
-        vd_turn(2, 0, 1)
-        vd_quant(1, 0, 2)
-        vd_out(2, 0, 0)
-        hidden_mm(1, 0)
-        vd_out(2, 0, 1)
-        spread_bl()
-        hidden_beta(1, 0)
-        hidden_mm(0, 1)
-        bl_out()
         vn_weave(3, 0, 0, A)
-        w_scale(1, 0)
-        vd_turn(2, 1, 0)
-        vd_turn(2, 1, 1)
-        hidden_beta(0, 1)
-        vd_out(2, 1, 0)
-        hidden_mm(1, 1)
-        vd_out(2, 1, 1)
-        w_scale(1, 1)
-        vd_turn(3, 0, 0)
-        hidden_sigmoid(0, 0, 0, 2)
-        vd_turn(3, 0, 1)
-        vd_quant(2, 0, 2)
-        vd_out(3, 0, 0)
-        vd_out(3, 0, 1)
-        w_weave(1, G)
-        hidden_beta(1, 1)
-        hidden_mm(0, 2)
-        hidden_signal(0, 0, 0, 2)
-        hidden_sigmoid(1, 0, 0, 2)
-        vd_turn(3, 1, 0)
-        vd_turn(3, 1, 1)
-        hidden_beta(0, 2)
-        vd_out(3, 1, 0)
-        hidden_mm(1, 2)
-        hidden_signal(1, 0, 0, 2)
-        vd_out(3, 1, 1)
-        g_turn(0, 0, 0, 2)
+        hidden_mm(0, 0)
+        vn_quant(0, 1)
+        vd_quant(1, 0, 1)
+        spread_bl()
+        vd_out(1, 1, 1)
+        keep_clock(3)
+        hidden_beta(0, 0)
         vn_weave(3, 0, 1, A)
-        hidden_beta(1, 2)
+        keep_clock(4)
+        vd_quant(1, 1, 2)
+        vd_turn(2, 0, 0)
+        w_scale(1, 0)
+        bl_out()
+        vn_weave(2, 0, 0, A)
+        vd_turn(2, 1, 0)
+        w_scale(1, 1)
+        hidden_mm(0, 1)
+        hidden_mm(1, 0)
+        vd_out(2, 0, 0)
+        hidden_beta(0, 1)
+        w_weave(1, G)
+        vd_turn(2, 0, 1)
+        vd_out(2, 1, 0)
+        hidden_beta(1, 0)
+        vd_turn(2, 1, 1)
+        hidden_sigmoid(0, 0, 0, 2)
+        hidden_mm(1, 1)
+        vd_out(2, 0, 1)
+        vd_turn(3, 0, 0)
+        hidden_signal(0, 0, 0, 2)
+        vd_out(2, 1, 1)
+        vd_turn(3, 0, 1)
+        vd_out(3, 0, 0)
+        hidden_beta(1, 1)
+        vd_turn(3, 1, 0)
+        vd_out(3, 0, 1)
+        vd_quant(2, 0, 2)
+        vd_turn(3, 1, 1)
+        vd_out(3, 1, 0)
+        keep_clock(5)
+        vd_out(3, 1, 1)
+        keep_clock(6)
+        vn_quant(3, 0)
+        hidden_mm(0, 2)
+        hidden_sigmoid(1, 0, 0, 2)
         vd_quant(3, 0, 2)
-        g_out(0, 0, 0, 2)
-        vn_weave(2, 1, 0, A)
+        g_turn(0, 0, 0, 2)
+        hidden_mm(1, 2)
+        vn_weave(2, 0, 1, A)
+        hidden_beta(0, 2)
         w_quant(1)
         hidden_mm(0, 3)
-        vn_quant(3, 0)
-        hidden_mm(2, 0)
-        w_weave(2, G)
-        hidden_beta(0, 3)
-        vn_weave(2, 1, 1, A)
-        hidden_beta(2, 0)
-        hidden_mm(1, 3)
-        hidden_sigmoid(0, 1, 0, 2)
-        hidden_mm(2, 1)
-        hidden_beta(1, 3)
-        g_turn(1, 0, 0, 2)
-        hidden_beta(2, 1)
-        hidden_sigmoid(1, 1, 0, 2)
-        hidden_mm(2, 2)
-        hidden_signal(0, 1, 0, 2)
-        hidden_mm(3, 2)
-        vn_weave(2, 0, 0, A)
-        hidden_beta(2, 2)
-        g_turn(0, 1, 0, 2)
-        hidden_beta(3, 2)
-        hidden_mm(3, 3)
-        hidden_sigmoid(2, 0, 0, 2)
-        vn_quant(2, 1)
-        hidden_mm(2, 3)
-        w_quant(2)
         vn_weave(1, 1, 0, A)
-        hidden_beta(3, 3)
-        w_weave(3, G)
-        hidden_beta(2, 3)
-        hidden_mm(3, 0)
-        g_out(0, 1, 0, 2)
-        hidden_signal(1, 1, 0, 2)
-        hidden_mm(3, 1)
-        g_out(1, 0, 0, 2)
-        hidden_signal(2, 0, 0, 2)
-        vn_weave(2, 0, 1, A)
-        g_turn(1, 1, 0, 2)
-        hidden_beta(3, 0)
-        g_out(1, 1, 0, 2)
-        hidden_beta(3, 1)
+        hidden_beta(1, 2)
+        keep_clock(7)
+        w_weave(2, G)
+        keep_clock(8)
+        hidden_beta(0, 3)
+        hidden_mm(1, 3)
+        g_out(0, 0, 0, 2)
+        hidden_signal(1, 0, 0, 2)
+        keep_clock(9)
+        hidden_mm(2, 2)
+        hidden_sigmoid(0, 1, 0, 2)
+        keep_clock(10)
+        hidden_beta(1, 3)
+        keep_clock(11)
+        keep_clock(12)
         vn_weave(1, 1, 1, A)
-        hidden_mm(5, 0)
-        g_quant(0, 0, 0, 2)
-        hidden_mm(5, 1)
-        g_quant(0, 1, 0, 2)
-        hidden_sigmoid(3, 1, 0, 2)
+        hidden_beta(2, 2)
+        g_turn(1, 0, 0, 2)
+        hidden_signal(0, 1, 0, 2)
+        hidden_mm(2, 3)
+        hidden_sigmoid(1, 1, 0, 2)
+        keep_clock(13)
+        keep_clock(14)
         vn_quant(2, 0)
-        grad_mm(0, 0, 0)
-        vn_weave(0, 1, 0, V)
+        hidden_mm(3, 0)
+        hidden_beta(2, 3)
+        g_out(1, 0, 0, 2)
+        keep_clock(15)
+        keep_clock(16)
+        w_quant(2)
+        keep_clock(17)
         hidden_sigmoid(2, 1, 0, 2)
-        grad_mm(0, 0, 3)
-        w_quant(3)
-        grad_out(0, 0, 0)
-        grad_out(0, 0, 3)
-        vn_quant(1, 1)
-        grad_mm(0, 0, 2)
-        vn_weave(3, 1, 0, A)
-        hidden_beta(5, 0)
-        grad_mm(0, 0, 1)
-        hidden_beta(5, 1)
-        hidden_mm(4, 0)
-        vn_weave(3, 1, 1, A)
+        hidden_mm(2, 0)
+        hidden_beta(3, 0)
+        w_weave(3, G)
+        keep_clock(18)
+        hidden_signal(1, 1, 0, 2)
+        keep_clock(19)
+        vn_weave(2, 1, 0, A)
+        hidden_mm(2, 1)
+        keep_clock(20)
+        hidden_beta(2, 0)
+        g_turn(0, 1, 0, 2)
+        vn_weave(2, 1, 1, A)
+        hidden_beta(2, 1)
+        g_turn(1, 1, 0, 2)
+        hidden_mm(3, 2)
         hidden_signal(2, 1, 0, 2)
-        hidden_mm(4, 1)
-        g_turn(2, 0, 0, 2)
-        grad_out(0, 0, 2)
-        hidden_beta(4, 0)
+        hidden_mm(3, 1)
+        g_out(0, 1, 0, 2)
+        keep_clock(21)
+        hidden_beta(3, 2)
+        g_out(1, 1, 0, 2)
         g_turn(2, 1, 0, 2)
-        hidden_sigmoid(3, 0, 0, 2)
-        vn_quant(0, 1)
+        hidden_beta(3, 1)
+        hidden_sigmoid(2, 0, 0, 2)
+        keep_clock(22)
+        g_quant(0, 0, 0, 2)
         hidden_mm(4, 2)
-        hidden_beta(4, 1)
-        g_out(2, 0, 0, 2)
-        vn_quant(3, 1)
-        grad_mm(0, 1, 0)
+        g_quant(0, 1, 0, 2)
+        hidden_sigmoid(3, 0, 0, 2)
+        hidden_mm(3, 3)
+        keep_clock(23)
+        vn_quant(1, 1)
+        grad_mm(0, 0, 1)
+        hidden_beta(3, 3)
+        grad_mm(0, 0, 0)
+        vn_weave(3, 1, 0, A)
+        hidden_beta(4, 2)
+        hidden_signal(2, 0, 0, 2)
+        hidden_mm(4, 0)
+        grad_out(0, 0, 0)
         grad_out(0, 0, 1)
+        hidden_mm(4, 1)
+        hidden_beta(4, 0)
+        vn_weave(3, 1, 1, A)
+        g_turn(2, 0, 0, 2)
+        hidden_beta(4, 1)
+        grad_mm(0, 0, 3)
+        hidden_signal(3, 0, 0, 2)
+        g_out(2, 1, 0, 2)
+        grad_mm(0, 0, 2)
+        hidden_sigmoid(3, 1, 0, 2)
+        hidden_mm(4, 3)
+        vn_quant(2, 1)
+        g_turn(3, 0, 0, 2)
+        hidden_beta(4, 3)
+        hidden_mm(5, 0)
+        grad_out(0, 0, 3)
+        grad_out(0, 0, 2)
+        vn_quant(3, 1)
+        hidden_mm(5, 1)
+        g_out(2, 0, 0, 2)
         hidden_signal(3, 1, 0, 2)
         grad_weave(0, 0, G)
         grad_store(0, 0)
-        hidden_mm(4, 3)
-        grad_out(0, 1, 0)
-        grad_mm(0, 1, 2)
-        hidden_beta(4, 2)
-        hidden_sigmoid(5, 0, 0, 2)
-        grad_mm(0, 1, 1)
-        hidden_beta(4, 3)
-        hidden_mm(5, 2)
-        hidden_signal(3, 0, 0, 2)
-        g_out(2, 1, 0, 2)
-        g_turn(3, 1, 0, 2)
-        grad_out(0, 1, 2)
-        hidden_beta(5, 2)
-        hidden_sigmoid(4, 0, 0, 2)
-        g_turn(3, 0, 0, 2)
-        hidden_signal(5, 0, 0, 2)
-        hidden_mm(6, 0)
-        g_out(3, 0, 0, 2)
-        grad_mm(0, 1, 3)
-        hidden_beta(6, 0)
-        g_out(3, 1, 0, 2)
-        hidden_mm(6, 1)
-        g_quant(1, 0, 0, 2)
-        grad_out(0, 1, 1)
-        hidden_mm(5, 3)
-        grad_out(0, 1, 3)
-        g_quant(1, 1, 0, 2)
+        grad_mm(0, 1, 0)
         hidden_sigmoid(4, 1, 0, 2)
+        grad_mm(0, 1, 3)
+        hidden_beta(5, 0)
+        g_turn(3, 1, 0, 2)
+        grad_out(0, 1, 0)
+        hidden_signal(4, 1, 0, 2)
+        g_out(3, 0, 0, 2)
+        hidden_mm(5, 2)
+        grad_out(0, 1, 3)
+        grad_mm(0, 1, 2)
+        g_out(3, 1, 0, 2)
+        hidden_beta(5, 1)
+        g_turn(4, 1, 0, 2)
+        g_quant(1, 0, 0, 2)
+        grad_out(0, 1, 2)
+        grad_mm(0, 1, 1)
+        hidden_sigmoid(4, 0, 0, 2)
+        g_quant(1, 1, 0, 2)
+        hidden_mm(5, 3)
+        hidden_beta(5, 2)
         grad_mm(1, 0, 0)
+        grad_out(0, 1, 1)
+        w_quant(3)
+        hidden_sigmoid(5, 0, 0, 2)
+        grad_mm(1, 0, 3)
         grad_store(0, 1)
         grad_weave(0, 1, G)
-        hidden_beta(6, 1)
-        grad_mm(1, 0, 1)
         hidden_beta(5, 3)
-        grad_out(1, 0, 0)
         hidden_mm(6, 2)
         hidden_signal(4, 0, 0, 2)
-        grad_out(1, 0, 1)
-        grad_mm(1, 0, 3)
-        hidden_sigmoid(5, 1, 0, 2)
-        grad_mm(1, 0, 2)
-        hidden_signal(4, 1, 0, 2)
-        g_turn(4, 0, 0, 2)
-        grad_out(1, 0, 3)
-        grad_out(1, 0, 2)
-        g_turn(5, 0, 0, 2)
-        hidden_beta(6, 2)
-        grad_mm(1, 1, 0)
-        g_out(4, 0, 0, 2)
-        grad_store(1, 0)
-        hidden_signal(5, 1, 0, 2)
-        g_out(5, 0, 0, 2)
-        grad_mm(1, 1, 2)
-        grad_out(1, 1, 0)
+        grad_out(1, 0, 0)
         hidden_mm(6, 3)
-        grad_out(1, 1, 2)
-        grad_quant(0, 0)
-        g_turn(4, 1, 0, 2)
-        g_quant(2, 0, 0, 2)
-        hidden_sigmoid(6, 0, 0, 2)
-        g_turn(5, 1, 0, 2)
-        grad_weave(1, 0, G)
-        hidden_beta(6, 3)
-        grad_mm(1, 1, 3)
-        g_out(4, 1, 0, 2)
+        grad_out(1, 0, 3)
+        hidden_sigmoid(5, 1, 0, 2)
+        grad_mm(1, 1, 0)
+        hidden_beta(6, 2)
         grad_mm(1, 1, 1)
-        hidden_signal(6, 0, 0, 2)
-        g_out(5, 1, 0, 2)
+        hidden_beta(6, 3)
+        g_out(4, 1, 0, 2)
+        g_turn(4, 0, 0, 2)
+        hidden_signal(5, 0, 0, 2)
+        grad_out(1, 1, 0)
         hidden_mm(7, 0)
-        grad_out(1, 1, 3)
-        hidden_mm(7, 1)
-        g_quant(2, 1, 0, 2)
         grad_out(1, 1, 1)
-        grad_mm(2, 1, 0)
+        g_out(4, 0, 0, 2)
+        hidden_mm(7, 1)
+        hidden_signal(5, 1, 0, 2)
         hidden_sigmoid(6, 1, 0, 2)
+        grad_mm(1, 1, 2)
+        grad_mm(1, 0, 1)
         hidden_beta(7, 0)
-        grad_store(1, 1)
-        grad_mm(2, 1, 3)
-        hidden_beta(7, 1)
-        grad_out(2, 1, 0)
-        hidden_mm(7, 2)
+        grad_out(1, 1, 2)
+        g_turn(5, 0, 0, 2)
         grad_quant(0, 1)
-        grad_out(2, 1, 3)
-        hidden_signal(6, 1, 0, 2)
-        grad_mm(2, 1, 2)
+        grad_out(1, 0, 1)
+        g_turn(5, 1, 0, 2)
+        hidden_beta(7, 1)
+        grad_mm(1, 0, 2)
+        g_out(5, 0, 0, 2)
+        g_out(5, 1, 0, 2)
+        grad_mm(1, 1, 3)
+        g_quant(2, 0, 0, 2)
+        grad_out(1, 0, 2)
+        hidden_mm(6, 0)
+        g_quant(2, 1, 0, 2)
+        grad_out(1, 1, 3)
+        hidden_mm(6, 1)
         hidden_sigmoid(7, 0, 0, 2)
-        grad_weave(1, 1, G)
-        code_store(0, 1)
+        grad_quant(0, 0)
+        grad_store(1, 1)
+        grad_store(1, 0)
         grad_mm(2, 0, 0)
-        hidden_beta(7, 2)
-        g_turn(6, 0, 0, 2)
-        grad_out(2, 1, 2)
+        grad_weave(1, 1, G)
+        hidden_beta(6, 0)
+        grad_mm(2, 0, 1)
+        hidden_beta(6, 1)
         grad_out(2, 0, 0)
-        g_turn(6, 1, 0, 2)
-        grad_mm(2, 1, 1)
-        grad_quant(1, 1)
-        g_out(6, 0, 0, 2)
-        grad_quant(1, 0)
-        g_out(6, 1, 0, 2)
+        hidden_mm(7, 2)
+        hidden_signal(6, 1, 0, 2)
+        grad_out(2, 0, 1)
+        grad_weave(1, 0, G)
         grad_mm(2, 0, 2)
-        g_quant(3, 0, 0, 2)
-        grad_out(2, 1, 1)
+        hidden_sigmoid(6, 0, 0, 2)
+        grad_mm(2, 0, 3)
+        hidden_beta(7, 2)
         hidden_mm(7, 3)
-        g_quant(3, 1, 0, 2)
         grad_out(2, 0, 2)
+        hidden_signal(6, 0, 0, 2)
+        grad_out(2, 0, 3)
+        grad_mm(2, 1, 0)
+        hidden_sigmoid(7, 1, 0, 1)
+        grad_mm(2, 1, 1)
+        grad_quant(1, 0)
+        grad_out(2, 1, 0)
+        grad_quant(1, 1)
+        g_turn(6, 0, 0, 2)
+        grad_out(2, 1, 1)
+        grad_weave(2, 0, G)
         hidden_signal(7, 0, 0, 2)
+        g_turn(6, 1, 0, 2)
+        code_store(1, 1)
+        grad_store(2, 0)
+        code_store(1, 0)
+        grad_mm(2, 1, 2)
+        g_out(6, 0, 0, 2)
+        g_out(6, 1, 0, 2)
+        hidden_beta(7, 3)
+        grad_mm(2, 1, 3)
+        grad_out(2, 1, 2)
+        g_quant(3, 0, 0, 2)
+        g_turn(7, 0, 0, 2)
+        grad_out(2, 1, 3)
+        g_quant(3, 1, 0, 2)
         grad_mm(3, 0, 0)
+        hidden_sigmoid(7, 1, 1, 2)
+        hidden_signal(7, 1, 0, 1)
         grad_weave(2, 1, G)
         grad_store(2, 1)
-        hidden_sigmoid(7, 1, 0, 1)
-        grad_mm(2, 0, 1)
-        grad_out(3, 0, 0)
-        hidden_beta(7, 3)
-        grad_mm(2, 0, 3)
-        grad_out(2, 0, 1)
-        grad_quant(2, 1)
-        grad_mm(3, 0, 3)
-        grad_out(2, 0, 3)
-        hidden_signal(7, 1, 0, 1)
-        g_turn(7, 0, 0, 2)
-        code_store(2, 1)
-        grad_out(3, 0, 3)
-        code_store(1, 1)
-        grad_mm(3, 0, 2)
-        grad_weave(2, 0, G)
-        grad_store(2, 0)
-        hidden_sigmoid(7, 1, 1, 2)
-        code_store(0, 0)
-        code_store(1, 0)
+        code_store(0, 1)
         grad_mm(3, 0, 1)
-        grad_out(3, 0, 2)
+        code_store(0, 0)
+        grad_out(3, 0, 0)
         hidden_signal(7, 1, 1, 2)
         grad_out(3, 0, 1)
-        grad_mm(3, 1, 0)
+        grad_mm(3, 0, 2)
         g_out(7, 0, 0, 2)
-        grad_mm(3, 1, 2)
-        grad_store(3, 0)
-        grad_weave(3, 0, V)
-        grad_out(3, 1, 0)
+        grad_mm(3, 0, 3)
+        grad_out(3, 0, 2)
         g_turn(7, 1, 0, 1)
-        grad_quant(2, 0)
-        grad_out(3, 1, 2)
+        grad_out(3, 0, 3)
         g_turn(7, 1, 1, 2)
-        g_quant(4, 0, 0, 2)
-        grad_mm(3, 1, 1)
-        g_out(7, 1, 0, 1)
-        code_store(2, 0)
+        grad_mm(3, 1, 0)
+        grad_weave(3, 0, V)
+        grad_store(3, 0)
         grad_mm(3, 1, 3)
-        g_out(7, 1, 1, 2)
-        g_quant(4, 1, 0, 1)
-        grad_mm(4, 1, 1, range(3), "beta_bank")
-        grad_out(3, 1, 1)
+        grad_quant(2, 1)
+        grad_out(3, 1, 0)
         grad_quant(3, 0)
         grad_out(3, 1, 3)
-        g_quant(4, 1, 1, 2)
-        grad_mm(4, 1, 2, range(3), "tr")
+        g_quant(4, 0, 0, 2)
+        grad_mm(3, 1, 2)
+        g_out(7, 1, 0, 1)
         code_store(3, 0)
+        grad_quant(2, 0)
+        grad_mm(3, 1, 1)
+        g_out(7, 1, 1, 2)
+        code_store(2, 1)
+        g_quant(4, 1, 0, 1)
+        grad_mm(4, 0, 2, range(3), "acc")
+        grad_out(3, 1, 2)
+        grad_out(3, 1, 1)
+        code_store(2, 0)
+        g_quant(4, 1, 1, 2)
+        grad_mm(4, 0, 0, range(3), "oacc0")
         grad_weave(3, 1, V)
         grad_store(3, 1)
+        grad_mm(4, 0, 3, range(3), "acc")
+        grad_mm(4, 0, 1, range(3), "oacc1")
+        grad_mm(4, 0, 1, range(3, 4))
+        grad_mm(4, 0, 0, range(3, 4))
+        grad_mm(4, 0, 2, range(3, 4))
+        grad_quant(3, 1)
+        grad_mm(4, 1, 2, range(3), "tr")
+        grad_out(4, 0, 0, "act")
+        grad_out(4, 0, 1, "dve")
+        grad_mm(4, 1, 3, range(3), "tr")
+        grad_out(4, 0, 2, "act")
+        code_store(3, 1)
+        grad_mm(4, 0, 3, range(3, 4))
+        scale_store_a()
         grad_mm(4, 1, 0, range(3), "beta_bank")
         grad_mm(4, 1, 0, range(3, 4))
+        grad_out(4, 0, 3, "dve")
         grad_mm(4, 1, 2, range(3, 4))
-        grad_mm(4, 1, 3, range(3), "tr")
+        grad_mm(4, 1, 1, range(3), "beta_bank")
         grad_out(4, 1, 0, "act")
         grad_mm(4, 1, 3, range(3, 4))
-        grad_quant(3, 1)
         grad_mm(4, 1, 1, range(3, 4))
-        grad_mm(4, 0, 3, range(3), "acc")
-        grad_out(4, 1, 2, "act")
-        grad_mm(4, 0, 3, range(3, 4))
-        grad_out(4, 1, 3, "act")
-        grad_out(4, 1, 1, "dve")
-        grad_mm(4, 0, 2, range(3), "acc")
-        scale_store_a()
-        grad_mm(4, 0, 0, range(3), "oacc")
-        code_store(3, 1)
-        grad_weave(4, 1, V)
-        grad_mm(4, 0, 0, range(3, 4))
-        grad_store(4, 1)
-        grad_mm(4, 0, 2, range(3, 4))
-        grad_mm(4, 0, 1, range(3), "oacc")
-        grad_out(4, 0, 0, "act")
-        grad_out(4, 0, 3, "dve")
-        grad_mm(4, 0, 1, range(3, 4))
-        grad_out(4, 0, 2, "act")
-        grad_quant(4, 1)
-        grad_out(4, 0, 1, "dve")
-        code_store(4, 1)
         grad_weave(4, 0, V)
         grad_store(4, 0)
+        grad_out(4, 1, 2, "act")
+        grad_out(4, 1, 3, "act")
+        grad_out(4, 1, 1, "dve")
+        grad_weave(4, 1, V)
+        grad_store(4, 1)
         grad_quant(4, 0)
+        grad_quant(4, 1)
         code_store(4, 0)
+        code_store(4, 1)
         scale_store_b()

from contextlib import ExitStack

import concourse.mybir as mybir
from concourse.masks import make_identity

F32 = mybir.dt.float32
BF16 = mybir.dt.bfloat16
U32 = mybir.dt.uint32
I32 = mybir.dt.int32
U8 = mybir.dt.uint8
FP8X4 = mybir.dt.float8_e4m3fn_x4
ALU = mybir.AluOpType
ACT = mybir.ActivationFunctionType

N = D = H = 1024
P = 128
PACK = 4
KP = P * PACK
GROUPS = 2
CHUNK = 256
CHUNKS = H // CHUNK
BLOCKS = 4
SPANS = [(0, 256), (256, 256), (512, 256), (768, 128), (896, 128)]
SPAN_OF = [0, 0, 1, 1, 2, 2, 3, 4]
LOSS_DIV = 32.0

TR_BUFS = 2
ACC_BUFS = 2
ZB = 3
GB = 2
WB = {"pool": 1, "act": 2, "dve": 2}
PB = {"oacc0": 1, "oacc1": 1, "acc": 2, "tr": 2, "beta_bank": 2}

FLOPS = 4 * 2 * N * D * H


def tile_gaussianrbmtwophasehiddenoffsetgrad_x1_kernel(tc, vpos, vneg, beta, u, c, b, lam, out_0, out_1, out_2):
    nc = tc.nc
    with ExitStack() as ctx:
        keep = ctx.enter_context(tc.tile_pool(name="keep", bufs=1))
        work = ctx.enter_context(tc.tile_pool(name="work", bufs=2))
        psum = ctx.enter_context(tc.psum_pool(name="psum", bufs=2))
        ctx.enter_context(tc.manual_schedule())

        def kept(name, shape, dtype):
            return keep.tile(shape, dtype, name=name, align_bytes=64)

        ident_f = kept("ident_f", [P, P], F32)
        ident_b = kept("ident_b", [P, P], BF16)
        c_raw = kept("c_raw", [P, GROUPS, PACK], BF16)
        c_in = kept("c_in", [P, GROUPS * PACK], F32)
        c_out = kept("c_out", [P, GROUPS * PACK], F32)
        beta_raw = kept("beta_raw", [P, BLOCKS, PACK], BF16)
        beta_sgn = kept("beta_sgn", [P, BLOCKS * PACK], BF16)
        beta_row = kept("beta_row", [P, BLOCKS, KP], BF16)
        bl_rows = kept("bl_rows", [P, P], BF16)
        bl_col = kept("bl_col", [P, 16], F32)
        warm = kept("warm", [P, 1], F32)
        u_raw = [kept("u_first", [P, GROUPS, PACK, CHUNK], BF16), kept("u_rest", [P, GROUPS, PACK, H - CHUNK], BF16)]
        w_scaled = u_raw
        v_raw = [kept("v_raw%d" % i, [P, PACK, D], BF16) for i in range(BLOCKS)]
        vd_codes = [kept("vd_codes%d" % i, [P, GROUPS, KP], U32) for i in range(BLOCKS)]
        vd_scales = [kept("vd_scales%d" % i, [P, GROUPS, KP], U8) for i in range(BLOCKS)]
        vn_codes = [kept("vn_codes%d" % i, [P, GROUPS, KP], U32) for i in range(BLOCKS)]
        vn_scales = [kept("vn_scales%d" % i, [P, GROUPS, KP], U8) for i in range(BLOCKS)]
        w_codes = [kept("w_codes%d" % i, [P, GROUPS, CHUNK], U32) for i in range(CHUNKS)]
        w_scales = [kept("w_scales%d" % i, [P, GROUPS, CHUNK], U8) for i in range(CHUNKS)]
        g_codes = {(sp, ph): kept("g_codes%d%d" % (sp, ph), [P, GROUPS, SPANS[sp][1]], U32) for sp in range(5) for ph in range(2)}
        g_scales = {(sp, ph): kept("g_scales%d%d" % (sp, ph), [P, GROUPS, SPANS[sp][1]], U8) for sp in range(5) for ph in range(2)}
        o_codes = kept("o_codes", [P, GROUPS, H], U32)
        o_scales = kept("o_scales", [P, GROUPS, H], U8)
        live = {}

        def v_rows(i):
            src = vpos if i < GROUPS else vneg
            g = i % GROUPS
            return src[g * KP:(g + 1) * KP, :].rearrange("(p j) d -> p j d", j=PACK)

        def load_u(part):
            cols = slice(0, CHUNK) if part == 0 else slice(CHUNK, H)
            for g in range(GROUPS):
                nc.sync.dma_start(out=u_raw[part][:, g, :, :], in_=u[g * KP:(g + 1) * KP, cols].rearrange("(p j) h -> p j h", j=PACK))

        def loads():
            nc.vector.memset(warm[:], 0.0)
            nc.vector.memset(bl_rows[:], 0.0)
            make_identity(nc, ident_f[:])
            make_identity(nc, ident_b[:])
            nc.sync.dma_start(out=v_raw[0][:, 0:2, 0:KP], in_=v_rows(0)[:, 0:2, 0:KP])
            nc.sync.dma_start(out=v_raw[0][:, 2:4, 0:KP], in_=v_rows(0)[:, 2:4, 0:KP])
            nc.scalar.dma_start(out=c_raw[:], in_=c.rearrange("(g p j) -> p g j", g=GROUPS, j=PACK))
            nc.scalar.dma_start(out=beta_raw[:], in_=beta.rearrange("f (g p j) -> p (f g) j", g=GROUPS, j=PACK))
            load_u(0)
            nc.sync.dma_start(out=v_raw[0][:, :, KP:D], in_=v_rows(0)[:, :, KP:D])
            nc.sync.dma_start(out=v_raw[1][:], in_=v_rows(1))
            nc.scalar.activation(out=warm[:], in_=warm[:], func=ACT.Sigmoid)
            nc.sync.dma_start(out=bl_rows[0:8, :], in_=b.rearrange("(r m) -> r m", m=P))
            nc.sync.dma_start(out=bl_rows[8:16, :], in_=lam.rearrange("(r m) -> r m", m=P))
            nc.sync.dma_start(out=v_raw[2][:], in_=v_rows(2))
            nc.sync.dma_start(out=v_raw[3][:], in_=v_rows(3))
            load_u(1)

        def small_vector():
            flat_c = c_raw[:].rearrange("p g j -> p (g j)")
            nc.vector.tensor_copy(out=c_in[:], in_=flat_c)
            nc.vector.tensor_scalar(out=c_out[:], in0=flat_c, scalar1=1.0 / LOSS_DIV, scalar2=None, op0=ALU.mult)
            flat_b = beta_raw[:].rearrange("p i j -> p (i j)")
            nc.vector.tensor_scalar(out=beta_sgn[:, 0:8], in0=flat_b[:, 0:8], scalar1=-1.0, scalar2=None, op0=ALU.mult)
            nc.vector.tensor_copy(out=beta_sgn[:, 8:16], in_=flat_b[:, 8:16])

        def spread_beta(ph):
            bank = psum.tile([P, 4, P], F32, name="beta_bank", bufs=2)
            live["beta_bank", ph] = bank
            words = beta_sgn[:].bitcast(F32)
            for k in range(4):
                w = 4 * ph + k
                nc.tensor.transpose(bank[:, k, :], words[:, w:w + 1].to_broadcast([P, P]), ident_f[:])

        def beta_out(ph):
            bank = live["beta_bank", ph]
            dst = beta_row[:, GROUPS * ph:GROUPS * (ph + 1), :].rearrange("p i n -> p (i n)").bitcast(F32)
            nc.scalar.copy(out=dst, in_=bank[:].rearrange("p k q -> p (k q)"))

        def spread_bl():
            bank = psum.tile([P, P], BF16, name="tr", bufs=TR_BUFS)
            nc.tensor.transpose(bank[:], bl_rows[:], ident_b[:])
            live["bl_bank"] = bank

        def bl_out():
            nc.scalar.copy(out=bl_col[:], in_=live["bl_bank"][:, 0:16])

        def pool_copy(out, in_):
            nc.gpsimd.tensor_scalar(out=out, in0=in_, scalar1=1.0, scalar2=0.0, op0=ALU.mult, op1=ALU.add)

        def act_copy(out, in_):
            nc.scalar.copy(out=out, in_=in_)

        def dve_copy(out, in_):
            nc.vector.tensor_copy(out=out, in_=in_)

        def lane(copy):
            return "pool" if copy is pool_copy else "act" if copy is act_copy else "dve"

        def w_scale(part, g):
            for j in range(PACK):
                k = PACK * g + j
                nc.vector.tensor_scalar(out=w_scaled[part][:, g, j, :], in0=u_raw[part][:, g, j, :], scalar1=c_in[:, k:k + 1], scalar2=None, op0=ALU.mult)

        def w_weave(hc, copy):
            src = w_scaled[0][:] if hc == 0 else w_scaled[1][:, :, :, (hc - 1) * CHUNK:hc * CHUNK]
            woven = work.tile([P, GROUPS, CHUNK, PACK], BF16, name="woven_" + lane(copy), bufs=WB[lane(copy)], align_bytes=64)
            copy(out=woven[:], in_=src.rearrange("p g j h -> p g h j"))
            live["w_woven", hc] = woven

        def w_quant(hc):
            nc.vector.quantize_mx(
                out=w_codes[hc][:].rearrange("p g h -> p (g h)").bitcast(FP8X4),
                scales=w_scales[hc][:].rearrange("p g h -> p (g h)"),
                in_=live["w_woven", hc][:].rearrange("p g h j -> p (g h j)"))

        def vd_turn(i, g, half):
            tag = "oacc1" if (4 * i + 2 * g + half) % 3 == 2 else "tr"
            bank = psum.tile([P, 2, 2, P], F32, name=tag, bufs=PB[tag])
            for e in range(2):
                words = v_raw[i][:, 2 * half + e, :].bitcast(F32)
                for w in range(2):
                    nc.tensor.transpose(bank[:, e, w, :], words[:, 256 * g + w:256 * (g + 1):2], ident_f[:])
            live["vd_bank", i, g, half] = bank

        def vd_out(i, g, half):
            if ("vd_woven", i) not in live:
                live["vd_woven", i] = work.tile([P, GROUPS, 2, P, 2, 2], F32, name="vd_woven", bufs=2, align_bytes=64)
            nc.scalar.copy(out=live["vd_woven", i][:, g, half, :, :, :], in_=live["vd_bank", i, g, half][:].rearrange("p e w q -> p q e w"))

        def vd_quant(i, lo, hi):
            nc.vector.quantize_mx(out=vd_codes[i][:, lo:hi, :].rearrange("p g n -> p (g n)").bitcast(FP8X4),
                                  scales=vd_scales[i][:, lo:hi, :].rearrange("p g n -> p (g n)"),
                                  in_=live["vd_woven", i][:, lo:hi].rearrange("p g a q e w -> p (g a q e w)").bitcast(BF16))

        def vn_weave(i, g, half, copy):
            if half == 0:
                live["vn_woven", i, g] = work.tile([P, PACK, P, PACK], BF16, name="woven_" + lane(copy), bufs=WB[lane(copy)], align_bytes=64)
            parts = 2 if copy is act_copy else 1
            ms = slice(half * P // parts, (half + 1) * P // parts)
            woven = live["vn_woven", i, g][:, :, ms, :]
            src = v_raw[i][:, :, g * KP + PACK * ms.start:g * KP + PACK * ms.stop]
            if copy is pool_copy:
                copy(out=woven.rearrange("p t m j -> p m j t"), in_=src.rearrange("p j (m t) -> p m j t", t=PACK))
            else:
                copy(out=woven.rearrange("p t (m a) j -> p m t a j", a=2), in_=src.rearrange("p j (m a t) -> p m t a j", a=2, t=PACK))

        def vn_quant(i, g):
            nc.vector.quantize_mx(out=vn_codes[i][:, g, :].bitcast(FP8X4), scales=vn_scales[i][:, g, :],
                                  in_=live["vn_woven", i, g][:].rearrange("p t m j -> p (t m j)"))

        def keep_clock(k):
            if "idle_bank" not in live:
                live["idle_bank"] = psum.tile([P, KP], F32, name="oacc0", bufs=1)
            nc.tensor.matmul_mx(out=live["idle_bank"][:], lhsT=vn_codes[0][:, 0, 0:P].bitcast(FP8X4), lhsT_scale=vn_scales[0][:, 0, 0:P],
                                rhs=vn_codes[0][:, 0, :].bitcast(FP8X4), rhs_scale=vn_scales[0][:, 0, :], start=True, stop=True)

        def hidden_mm(ht, i):
            hc, a = divmod(ht, 2)
            acc = psum.tile([P, KP], F32, name="acc", bufs=ACC_BUFS)
            cols = slice(a * P, (a + 1) * P)
            for g in range(GROUPS):
                nc.tensor.matmul_mx(out=acc[:], lhsT=w_codes[hc][:, g, cols].bitcast(FP8X4), lhsT_scale=w_scales[hc][:, g, cols],
                                    rhs=vd_codes[i][:, g, :].bitcast(FP8X4), rhs_scale=vd_scales[i][:, g, :],
                                    start=(g == 0), stop=(g == GROUPS - 1))
            live["acc", ht, i] = acc

        def hidden_beta(ht, i):
            ph, g = divmod(i, GROUPS)
            if ("z", ht, ph) not in live:
                live["z", ht, ph] = work.tile([P, GROUPS, KP], F32, name="z", bufs=ZB)
            nc.vector.tensor_tensor(out=live["z", ht, ph][:, g, :], in0=live["acc", ht, i][:], in1=beta_row[:, i, :], op=ALU.mult)

        def flat(tile, lo, hi):
            return tile[:, lo:hi, :].rearrange("p g n -> p (g n)")

        def hidden_sigmoid(ht, ph, lo, hi):
            if ("s", ht, ph) not in live:
                live["s", ht, ph] = work.tile([P, GROUPS, KP], F32, name="s", bufs=ZB)
            nc.scalar.activation(out=flat(live["s", ht, ph], lo, hi), in_=flat(live["z", ht, ph], lo, hi), func=ACT.Sigmoid,
                                 bias=bl_col[:, ht:ht + 1], scale=(-1.0 if ph == 0 else 1.0))

        def hidden_signal(ht, ph, lo, hi):
            if ("gt", ht, ph) not in live:
                live["gt", ht, ph] = work.tile([P, GROUPS, KP], BF16, name="gt", bufs=ZB)
            beta_bf = live["beta_bank", ph][:, 2 * lo:2 * hi, :].rearrange("p k q -> p (k q)").bitcast(BF16)
            nc.vector.scalar_tensor_tensor(out=flat(live["gt", ht, ph], lo, hi), in0=flat(live["s", ht, ph], lo, hi),
                                           scalar=bl_col[:, 8 + ht:9 + ht], in1=beta_bf, op0=ALU.subtract, op1=ALU.mult)

        def g_turn(ht, ph, lo, hi):
            bank = psum.tile([P, hi - lo, 2, P], F32, name="tr", bufs=TR_BUFS)
            for g in range(lo, hi):
                words = live["gt", ht, ph][:, g, :].bitcast(F32)
                for w in range(2):
                    nc.tensor.transpose(bank[:, g - lo, w, :], words[:, w * P:(w + 1) * P], ident_f[:])
            live["g_bank", ht, ph, lo] = bank

        def g_out(ht, ph, lo, hi):
            sp = SPAN_OF[ht]
            first, width = SPANS[sp]
            if ("g_woven", sp, ph) not in live:
                live["g_woven", sp, ph] = work.tile([P, GROUPS, width, 2], F32, name="g_woven", bufs=GB, align_bytes=64)
            at = ht * P - first
            nc.scalar.copy(out=live["g_woven", sp, ph][:, lo:hi, at:at + P, :], in_=live["g_bank", ht, ph, lo][:].rearrange("p g w h -> p g h w"))

        def g_quant(sp, ph, lo, hi):
            nc.vector.quantize_mx(out=flat(g_codes[sp, ph], lo, hi).bitcast(FP8X4), scales=flat(g_scales[sp, ph], lo, hi),
                                  in_=live["g_woven", sp, ph][:, lo:hi].rearrange("p g h w -> p (g h w)").bitcast(BF16))

        def grad_mm(sp, g, t, blocks=range(BLOCKS), tag=None):
            if blocks[0] == 0:
                live["oacc", sp, g, t] = psum.tile([P, SPANS[sp][1]], F32, name=tag or "oacc%d" % (t % 2), bufs=PB[tag or "oacc0"])
            acc = live["oacc", sp, g, t]
            rows = slice(t * P, (t + 1) * P)
            for i in blocks:
                ph, ng = divmod(i, GROUPS)
                nc.tensor.matmul_mx(out=acc[:], lhsT=vn_codes[i][:, g, rows].bitcast(FP8X4), lhsT_scale=vn_scales[i][:, g, rows],
                                    rhs=g_codes[sp, ph][:, ng, :].bitcast(FP8X4), rhs_scale=g_scales[sp, ph][:, ng, :],
                                    start=(i == 0), stop=(i == BLOCKS - 1))

        def grad_out(sp, g, t, on="act"):
            if ("res", sp, g) not in live:
                live["res", sp, g] = work.tile([P, PACK, SPANS[sp][1]], F32, name="res", bufs=3)
            k = PACK * g + t
            if on == "act":
                nc.scalar.activation(out=live["res", sp, g][:, t, :], in_=live["oacc", sp, g, t][:], func=ACT.Copy, scale=c_out[:, k:k + 1])
            else:
                nc.vector.tensor_scalar(out=live["res", sp, g][:, t, :], in0=live["oacc", sp, g, t][:], scalar1=c_out[:, k:k + 1], scalar2=None, op0=ALU.mult)

        def grad_store(sp, g):
            cols = slice(SPANS[sp][0], SPANS[sp][0] + SPANS[sp][1])
            nc.sync.dma_start(out=out_0[g * KP:(g + 1) * KP, cols].rearrange("(p t) m -> p t m", t=PACK), in_=live["res", sp, g][:])

        def grad_weave(sp, g, copy):
            woven = work.tile([P, SPANS[sp][1], PACK], BF16, name="res_woven_%s%d" % (lane(copy), g), bufs=1, align_bytes=64)
            copy(out=woven[:], in_=live["res", sp, g][:].rearrange("p t m -> p m t"))
            live["res_woven", sp, g] = woven

        def grad_quant(sp, g):
            cols = slice(SPANS[sp][0], SPANS[sp][0] + SPANS[sp][1])
            nc.vector.quantize_mx(out=o_codes[:, g, cols].bitcast(FP8X4), scales=o_scales[:, g, cols],
                                  in_=live["res_woven", sp, g][:].rearrange("p m t -> p (m t)"))

        def code_store(sp, g):
            cols = slice(SPANS[sp][0], SPANS[sp][0] + SPANS[sp][1])
            nc.sync.dma_start(out=out_1[g, :, cols, :].rearrange("p m t -> p (m t)").bitcast(I32), in_=o_codes[:, g, cols].bitcast(I32))

        def scale_store(lo, hi, queues):
            for q in range(4):
                queues[q % len(queues)].dma_start(
                    out=out_2[:, 4 * q:4 * q + 4, lo:hi].rearrange("g r m -> r g m").bitcast(I32),
                    in_=o_scales[32 * q:32 * q + 4, :, lo:hi].bitcast(I32))

        def scale_store_a():
            scale_store(0, 896, [nc.sync])

        def scale_store_b():
            scale_store(896, 1024, [nc.sync, nc.scalar])

        G, A, V = pool_copy, act_copy, dve_copy
        loads()
        small_vector()
        vd_turn(0, 0, 0)
        vn_weave(0, 0, 0, V)
        vd_turn(0, 0, 1)
        vd_out(0, 0, 0)
        spread_beta(1)
        vn_quant(0, 0)
        vd_out(0, 0, 1)
        w_scale(0, 0)
        keep_clock(0)
        beta_out(1)
        w_scale(0, 1)
        keep_clock(1)
        vd_quant(0, 0, 1)
        keep_clock(2)
        w_weave(0, V)
        vd_turn(0, 1, 0)
        vn_weave(1, 0, 0, V)
        vd_turn(0, 1, 1)
        vd_out(0, 1, 0)
        vd_turn(1, 0, 0)
        w_quant(0)
        vd_out(0, 1, 1)
        spread_beta(0)
        vd_turn(1, 0, 1)
        vd_out(1, 0, 0)
        vd_quant(0, 1, 2)
        vd_turn(1, 1, 0)
        beta_out(0)
        vn_weave(0, 1, 0, V)
        vd_out(1, 0, 1)
        vd_turn(1, 1, 1)
        vd_out(1, 1, 0)
        vn_quant(1, 0)
        vn_weave(3, 0, 0, A)
        hidden_mm(0, 0)
        vn_quant(0, 1)
        vd_quant(1, 0, 1)
        spread_bl()
        vd_out(1, 1, 1)
        keep_clock(3)
        hidden_beta(0, 0)
        vn_weave(3, 0, 1, A)
        keep_clock(4)
        vd_quant(1, 1, 2)
        vd_turn(2, 0, 0)
        w_scale(1, 0)
        bl_out()
        vn_weave(2, 0, 0, A)
        vd_turn(2, 1, 0)
        w_scale(1, 1)
        hidden_mm(0, 1)
        hidden_mm(1, 0)
        vd_out(2, 0, 0)
        hidden_beta(0, 1)
        w_weave(1, G)
        vd_turn(2, 0, 1)
        vd_out(2, 1, 0)
        hidden_beta(1, 0)
        vd_turn(2, 1, 1)
        hidden_sigmoid(0, 0, 0, 2)
        hidden_mm(1, 1)
        vd_out(2, 0, 1)
        vd_turn(3, 0, 0)
        hidden_signal(0, 0, 0, 2)
        vd_out(2, 1, 1)
        vd_turn(3, 0, 1)
        vd_out(3, 0, 0)
        hidden_beta(1, 1)
        vd_turn(3, 1, 0)
        vd_out(3, 0, 1)
        vd_quant(2, 0, 2)
        vd_turn(3, 1, 1)
        vd_out(3, 1, 0)
        keep_clock(5)
        vd_out(3, 1, 1)
        keep_clock(6)
        vn_quant(3, 0)
        hidden_mm(0, 2)
        hidden_sigmoid(1, 0, 0, 2)
        vd_quant(3, 0, 2)
        g_turn(0, 0, 0, 2)
        hidden_mm(1, 2)
        vn_weave(2, 0, 1, A)
        hidden_beta(0, 2)
        w_quant(1)
        hidden_mm(0, 3)
        vn_weave(1, 1, 0, A)
        hidden_beta(1, 2)
        keep_clock(7)
        w_weave(2, G)
        keep_clock(8)
        hidden_beta(0, 3)
        hidden_mm(1, 3)
        g_out(0, 0, 0, 2)
        hidden_signal(1, 0, 0, 2)
        keep_clock(9)
        hidden_mm(2, 2)
        hidden_sigmoid(0, 1, 0, 2)
        keep_clock(10)
        hidden_beta(1, 3)
        keep_clock(11)
        keep_clock(12)
        vn_weave(1, 1, 1, A)
        hidden_beta(2, 2)
        g_turn(1, 0, 0, 2)
        hidden_signal(0, 1, 0, 2)
        hidden_mm(2, 3)
        hidden_sigmoid(1, 1, 0, 2)
        keep_clock(13)
        keep_clock(14)
        vn_quant(2, 0)
        hidden_mm(3, 0)
        hidden_beta(2, 3)
        g_out(1, 0, 0, 2)
        keep_clock(15)
        keep_clock(16)
        w_quant(2)
        keep_clock(17)
        hidden_sigmoid(2, 1, 0, 2)
        hidden_mm(2, 0)
        hidden_beta(3, 0)
        w_weave(3, G)
        keep_clock(18)
        hidden_signal(1, 1, 0, 2)
        keep_clock(19)
        vn_weave(2, 1, 0, A)
        hidden_mm(2, 1)
        keep_clock(20)
        hidden_beta(2, 0)
        g_turn(0, 1, 0, 2)
        vn_weave(2, 1, 1, A)
        hidden_beta(2, 1)
        g_turn(1, 1, 0, 2)
        hidden_mm(3, 2)
        hidden_signal(2, 1, 0, 2)
        hidden_mm(3, 1)
        g_out(0, 1, 0, 2)
        keep_clock(21)
        hidden_beta(3, 2)
        g_out(1, 1, 0, 2)
        g_turn(2, 1, 0, 2)
        hidden_beta(3, 1)
        hidden_sigmoid(2, 0, 0, 2)
        keep_clock(22)
        g_quant(0, 0, 0, 2)
        hidden_mm(4, 2)
        g_quant(0, 1, 0, 2)
        hidden_sigmoid(3, 0, 0, 2)
        hidden_mm(3, 3)
        keep_clock(23)
        vn_quant(1, 1)
        grad_mm(0, 0, 1)
        hidden_beta(3, 3)
        grad_mm(0, 0, 0)
        vn_weave(3, 1, 0, A)
        hidden_beta(4, 2)
        hidden_signal(2, 0, 0, 2)
        hidden_mm(4, 0)
        grad_out(0, 0, 0)
        grad_out(0, 0, 1)
        hidden_mm(4, 1)
        hidden_beta(4, 0)
        vn_weave(3, 1, 1, A)
        g_turn(2, 0, 0, 2)
        hidden_beta(4, 1)
        grad_mm(0, 0, 3)
        hidden_signal(3, 0, 0, 2)
        g_out(2, 1, 0, 2)
        grad_mm(0, 0, 2)
        hidden_sigmoid(3, 1, 0, 2)
        hidden_mm(4, 3)
        vn_quant(2, 1)
        g_turn(3, 0, 0, 2)
        hidden_beta(4, 3)
        hidden_mm(5, 0)
        grad_out(0, 0, 3)
        grad_out(0, 0, 2)
        vn_quant(3, 1)
        hidden_mm(5, 1)
        g_out(2, 0, 0, 2)
        hidden_signal(3, 1, 0, 2)
        grad_weave(0, 0, G)
        grad_store(0, 0)
        grad_mm(0, 1, 0)
        hidden_sigmoid(4, 1, 0, 2)
        grad_mm(0, 1, 3)
        hidden_beta(5, 0)
        g_turn(3, 1, 0, 2)
        grad_out(0, 1, 0)
        hidden_signal(4, 1, 0, 2)
        g_out(3, 0, 0, 2)
        hidden_mm(5, 2)
        grad_out(0, 1, 3)
        grad_mm(0, 1, 2)
        g_out(3, 1, 0, 2)
        hidden_beta(5, 1)
        g_turn(4, 1, 0, 2)
        g_quant(1, 0, 0, 2)
        grad_out(0, 1, 2)
        grad_mm(0, 1, 1)
        hidden_sigmoid(4, 0, 0, 2)
        g_quant(1, 1, 0, 2)
        hidden_mm(5, 3)
        hidden_beta(5, 2)
        grad_mm(1, 0, 0)
        grad_out(0, 1, 1)
        w_quant(3)
        hidden_sigmoid(5, 0, 0, 2)
        grad_mm(1, 0, 3)
        grad_store(0, 1)
        grad_weave(0, 1, G)
        hidden_beta(5, 3)
        hidden_mm(6, 2)
        hidden_signal(4, 0, 0, 2)
        grad_out(1, 0, 0)
        hidden_mm(6, 3)
        grad_out(1, 0, 3)
        hidden_sigmoid(5, 1, 0, 2)
        grad_mm(1, 1, 0)
        hidden_beta(6, 2)
        grad_mm(1, 1, 1)
        hidden_beta(6, 3)
        g_out(4, 1, 0, 2)
        g_turn(4, 0, 0, 2)
        hidden_signal(5, 0, 0, 2)
        grad_out(1, 1, 0)
        hidden_mm(7, 0)
        grad_out(1, 1, 1)
        g_out(4, 0, 0, 2)
        hidden_mm(7, 1)
        hidden_signal(5, 1, 0, 2)
        hidden_sigmoid(6, 1, 0, 2)
        grad_mm(1, 1, 2)
        grad_mm(1, 0, 1)
        hidden_beta(7, 0)
        grad_out(1, 1, 2)
        g_turn(5, 0, 0, 2)
        grad_quant(0, 1)
        grad_out(1, 0, 1)
        g_turn(5, 1, 0, 2)
        hidden_beta(7, 1)
        grad_mm(1, 0, 2)
        g_out(5, 0, 0, 2)
        g_out(5, 1, 0, 2)
        grad_mm(1, 1, 3)
        g_quant(2, 0, 0, 2)
        grad_out(1, 0, 2)
        hidden_mm(6, 0)
        g_quant(2, 1, 0, 2)
        grad_out(1, 1, 3)
        hidden_mm(6, 1)
        hidden_sigmoid(7, 0, 0, 2)
        grad_quant(0, 0)
        grad_store(1, 1)
        grad_store(1, 0)
        grad_mm(2, 0, 0)
        grad_weave(1, 1, G)
        hidden_beta(6, 0)
        grad_mm(2, 0, 1)
        hidden_beta(6, 1)
        grad_out(2, 0, 0)
        hidden_mm(7, 2)
        hidden_signal(6, 1, 0, 2)
        grad_out(2, 0, 1)
        grad_weave(1, 0, G)
        grad_mm(2, 0, 2)
        hidden_sigmoid(6, 0, 0, 2)
        grad_mm(2, 0, 3)
        hidden_beta(7, 2)
        hidden_mm(7, 3)
        grad_out(2, 0, 2)
        hidden_signal(6, 0, 0, 2)
        grad_out(2, 0, 3)
        grad_mm(2, 1, 0)
        hidden_sigmoid(7, 1, 0, 1)
        grad_mm(2, 1, 1)
        grad_quant(1, 0)
        grad_out(2, 1, 0)
        grad_quant(1, 1)
        g_turn(6, 0, 0, 2)
        grad_out(2, 1, 1)
        grad_weave(2, 0, G)
        hidden_signal(7, 0, 0, 2)
        g_turn(6, 1, 0, 2)
        code_store(1, 1)
        grad_store(2, 0)
        code_store(1, 0)
        grad_mm(2, 1, 2)
        g_out(6, 0, 0, 2)
        g_out(6, 1, 0, 2)
        hidden_beta(7, 3)
        grad_mm(2, 1, 3)
        grad_out(2, 1, 2)
        g_quant(3, 0, 0, 2)
        g_turn(7, 0, 0, 2)
        grad_out(2, 1, 3)
        g_quant(3, 1, 0, 2)
        grad_mm(3, 0, 0)
        hidden_sigmoid(7, 1, 1, 2)
        hidden_signal(7, 1, 0, 1)
        grad_weave(2, 1, G)
        grad_store(2, 1)
        code_store(0, 1)
        grad_mm(3, 0, 1)
        code_store(0, 0)
        grad_out(3, 0, 0)
        hidden_signal(7, 1, 1, 2)
        grad_out(3, 0, 1)
        grad_mm(3, 0, 2)
        g_out(7, 0, 0, 2)
        grad_mm(3, 0, 3)
        grad_out(3, 0, 2)
        g_turn(7, 1, 0, 1)
        grad_out(3, 0, 3)
        g_turn(7, 1, 1, 2)
        grad_mm(3, 1, 0)
        grad_weave(3, 0, V)
        grad_store(3, 0)
        grad_mm(3, 1, 3)
        grad_quant(2, 1)
        grad_out(3, 1, 0)
        grad_quant(3, 0)
        grad_out(3, 1, 3)
        g_quant(4, 0, 0, 2)
        grad_mm(3, 1, 2)
        g_out(7, 1, 0, 1)
        code_store(3, 0)
        grad_quant(2, 0)
        grad_mm(3, 1, 1)
        g_out(7, 1, 1, 2)
        code_store(2, 1)
        g_quant(4, 1, 0, 1)
        grad_mm(4, 0, 2, range(3), "acc")
        grad_out(3, 1, 2)
        grad_out(3, 1, 1)
        code_store(2, 0)
        g_quant(4, 1, 1, 2)
        grad_mm(4, 0, 0, range(3), "oacc0")
        grad_weave(3, 1, V)
        grad_store(3, 1)
        grad_mm(4, 0, 3, range(3), "acc")
        grad_mm(4, 0, 1, range(3), "oacc1")
        grad_mm(4, 0, 1, range(3, 4))
        grad_mm(4, 0, 0, range(3, 4))
        grad_mm(4, 0, 2, range(3, 4))
        grad_quant(3, 1)
        grad_mm(4, 1, 2, range(3), "tr")
        grad_out(4, 0, 0, "act")
        grad_out(4, 0, 1, "dve")
        grad_mm(4, 1, 3, range(3), "tr")
        grad_out(4, 0, 2, "act")
        code_store(3, 1)
        grad_mm(4, 0, 3, range(3, 4))
        scale_store_a()
        grad_mm(4, 1, 0, range(3), "beta_bank")
        grad_mm(4, 1, 0, range(3, 4))
        grad_out(4, 0, 3, "dve")
        grad_mm(4, 1, 2, range(3, 4))
        grad_mm(4, 1, 1, range(3), "beta_bank")
        grad_out(4, 1, 0, "act")
        grad_mm(4, 1, 3, range(3, 4))
        grad_mm(4, 1, 1, range(3, 4))
        grad_weave(4, 0, V)
        grad_store(4, 0)
        grad_out(4, 1, 2, "act")
        grad_out(4, 1, 3, "act")
        grad_out(4, 1, 1, "dve")
        grad_weave(4, 1, V)
        grad_store(4, 1)
        grad_quant(4, 0)
        grad_quant(4, 1)
        code_store(4, 0)
        code_store(4, 1)
        scale_store_b()
